import numpy as np, ml_dtypes
CORES = [5,29,101,125,133,157,229,253]
N = 8
import mx_ref
BF = ml_dtypes.bfloat16
def gcols(t, e):
    v = np.concatenate([t.reshape(8, 16, -1, 4), np.zeros((8, 16, 1, 4), BF)], axis=2)
    return np.ascontiguousarray(np.stack([v[g][:, e[g]] for g in range(8)])).reshape(128, -1)
def tile(rs):
    return np.stack(rs, axis=2).reshape(128, -1).astype(BF)
def cut(t, i, w=512):
    return t[:, w * i:w * i + w]
def pick(q, e):
    c = np.concatenate([q[0].reshape(128, -1, 4), np.zeros((128, 1, 4), np.uint8)], axis=1); s = np.concatenate([q[1], np.ones((16, 1), np.uint8)], axis=1)
    return (np.ascontiguousarray(c[:, e].reshape(128, -1)), np.ascontiguousarray(s[:, e]))
def join(*qs):
    return (np.concatenate([q[0] for q in qs], axis=1), np.concatenate([q[1] for q in qs], axis=1))
def put(q, e, v):
    c, s = q[0].reshape(128, -1, 4).copy(), q[1].copy(); c[:, e] = v[0].reshape(128, -1, 4); s[:, e] = v[1]
    return (c.reshape(128, -1), s)
def pk(c, s):
    return (np.ascontiguousarray(c), mx_ref.live(s))
def emit(q):
    return q[0], q[1]
def packed(v, rng):
    q = [mx_ref.quantize(np.ascontiguousarray(v[r])) for r in range(N)]
    return np.stack([a for a, b in q]), np.stack([mx_ref.plane(b, rng) for a, b in q])
def values_of_codes():
    e, c = np.zeros((128, 128, 4), np.float32), np.zeros((128, 2, 4), np.uint8)
    e[np.arange(128), np.arange(128), 0] = 1
    c[:127, :, 0] = np.arange(256).reshape(2, 128).T[:127]
    return mx_ref.matmul(mx_ref.quantize(e.reshape(128, 512).astype(BF)), (c.reshape(128, 8), np.full((16, 2), 127, np.uint8))).T.reshape(-1).astype(np.float64)
CODE_VALUE, SCALE_VALUE = values_of_codes(), 2.0 ** (np.arange(256) - 127.0)
def decode(q):
    return (CODE_VALUE[q[0]].reshape(16, 8, -1, 4) * SCALE_VALUE[q[1]][:, None, :, None] + 0.0).reshape(128, -1).astype(np.float32)
def f(rng, *shape):
    return mx_ref.flush((rng.standard_normal(shape, dtype=np.float32) * np.exp2(rng.integers(-2, 3, shape[:-1] + (1,)))).astype(BF))
def wide(rng, *shape, cols=0):
    v = rng.standard_normal(shape, dtype=np.float32) * np.exp2(rng.integers(-12, 13, shape)).astype(np.float32)
    if cols: v *= np.repeat(np.exp2(rng.integers(-cols, cols + 1, shape[:-2] + (1, shape[-1] // 4))) * (rng.random(shape[:-2] + (1, shape[-1] // 4)) > 0.0625), 4, axis=-1).astype(np.float32)
    return mx_ref.flush(v.astype(BF))
C, S, R = 416, 64, 2
STEP = [4, 1]
def partner(r, t):
    return r ^ STEP[t]
def order(p):
    return np.argsort(-(p[::16] + np.float32(0.0)), axis=1, kind="stable")
def walk(pi):
    g, p = np.arange(8), np.zeros(8, int)
    e, taken = np.zeros((8, C), int), np.zeros((8, C), bool)
    for k in range(C):
        e[:, k] = p
        taken[g, p] = True
        p = pi[g, p]
        p = np.where(taken[g, p], np.argmin(taken, axis=1), p)
    return e
def common(w, rng):
    c, p = packed(np.stack([w] * N), rng)
    return {"wc": c, "ws": p}
def weights(rng, keep=()):
    w = np.array(f(rng, 128, 2048)).reshape(128, 4, 8, 16, 4)
    for p in keep: w[:, :, :, p] = 0
    if len(keep): w[::16] = 0
    return common(w.reshape(128, 2048), rng)
def numbers_of(rng):
    return {"x": np.array(f(rng, N, 128, 4 * C)), "u": np.stack([f(rng, 128, 512)] * N), "v": np.array(f(rng, N, 128, 512))}
def planted(rng, s, sign, kind):
    d = numbers_of(rng)
    x = d["x"].astype(np.float32).reshape(N, 8, 16, C, 4)
    digit = ((s[:, :, :, None] >> np.arange(12)) & 1) * np.exp2(np.arange(12) - 23.0)
    x[:, :, 0] = 0
    x[:, :, 0, :, 0] = sign[:, :, None]
    for a in range(3): x[:, :, 8 + a] = digit[:, :, :, 4 * a:4 * a + 4]
    x[:, :, 11:] = rng.integers(4, 8, (N, 8, 5, C, 4)) * rng.choice([-1.0, 1.0], (N, 8, 5, C, 4)) * 2.0 ** -20
    u = d["u"].reshape(N, 128, 128, 4)
    u[:, :, ::16] = 0
    for g in range(8):
        k = 1.0 if kind[g] < 2 else 2.0 ** -30
        u[:, 16 * g, 16 * g, 0] = k
        u[:, 16 * g + 8:16 * g + 11, 16 * g] = k
        if kind[g] == 1: x[:, g, 0, int(rng.integers(C)), 0] *= 2.0 ** 30
        if kind[g] == 3:
            x[:, g, 0] = 0
            x[:, g, 8:] *= 2.0 ** -7
            x[:, g, 8:11] *= sign[:, g][:, None, None, None]
            x[:, g, 11] = 0
            u[:, 16 * g + 11, 16 * g, 0] = 1.125 * k
            u[:, 16 * g + 11, 16 * g, 1] = k
            for r in range(N):
                if r & STEP[0]:
                    j = int(np.flatnonzero(s[r, g] == 0)[-1])
                    x[r, g, 11, j, 0] = 1.125 * 2.0 ** -30
                    x[r, g, 11, j, 1] = -1.25 * 2.0 ** -30
    return {"x": x.reshape(N, 128, 4 * C).astype(BF), "u": u.reshape(N, 128, 512), "v": d["v"], **weights(rng, [0] + [*range(8, 16)])}
def setup_inputs(rng):
    return {**numbers_of(rng), **weights(rng)}
def setup_inputs_ties(rng):
    d = numbers_of(rng)
    e = rng.permutation(N)
    x = d["x"].reshape(N, 8, 16, C, 4)
    for r in range(N):
        for g in range(8):
            k = np.zeros(C, int) if r == e[0] else rng.permutation(C) % 3
            a = x[r, g, :8, :3].copy()
            a[:, 2] = 0
            x[r, g, :8] = a[:, k]
    x[e[1]] = 0
    u = d["u"].reshape(N, 8, 16, 128, 4)
    for g in range(8):
        own = u[:, g, :8, 16 * g].copy()
        u[:, :, :, 16 * g] = 0
        u[:, g, :8, 16 * g] = own
    return {"x": x.reshape(N, 128, 4 * C), "u": u.reshape(N, 128, 512), "v": d["v"], **weights(rng, [*range(8)])}
def setup_inputs_near(rng):
    s = np.stack([np.stack([rng.permutation(C) // 2 for g in range(8)]) for r in range(N)])
    sign = np.stack([rng.permutation(8) % 2 * 2.0 - 1.0 for r in range(N)])
    return planted(rng, s, sign, rng.permutation(8) % 4)
def setup_inputs_cycles(rng):
    size = [[C], [257] + [1] * (C - 257), [2] * (C // 2), [3] * (C // 3) + [1] * (C % 3)]
    s = np.zeros((N, 8, C), int)
    h = rng.permutation(8)
    for q in range(N):
        if q & (STEP[0] | STEP[1]): continue
        for g in range(8):
            i, m, pi, at = rng.permutation(C), rng.permutation(C), np.zeros(C, int), 0
            if h[g] // 2 == 0:
                m = np.roll(m, -int(np.argmin(m)))
                m[1:3] = np.sort(m[1:3])
                m[-2:] = np.sort(m[-2:])[::-1]
            for n in size[h[g] // 2]:
                pi[m[at:at + n]] = np.roll(m[at:at + n], -1)
                at += n
            other = i.copy()
            if h[g] == 4:
                k = pi[np.flatnonzero(pi > np.arange(C))[-2:]]
                other[k] = i[k[::-1]]
            for r in (q, q ^ STEP[0], q ^ STEP[1], q ^ STEP[0] ^ STEP[1]):
                c = other if r & STEP[1] else i
                s[r, g] = C - 1 - (c[pi] if r & STEP[h[g] % 2] else c)
    sign = np.tile(rng.permutation(8) % 2 * 2.0 - 1.0, (N, 1))
    return planted(rng, s, sign, rng.permutation(8) % 2 * 2)
def setup_inputs_huge(rng):
    d = numbers_of(rng)
    x = 2.0 ** 30 * (0.9 + 0.1 * rng.random((N, 128, C, 4)))
    x[:, ::8, :, 0] = 2.0 ** 30
    c = np.stack([rng.permutation(C) % 2 * 2.0 - 1.0 for r in range(N)])
    c[rng.permutation(N) < N // 2] = 1
    x *= c[:, None, :, None]
    u = d["u"].reshape(N, 128, 128, 4)
    a = 2.0 ** 30 * (1 - 0.1 * rng.random((128, 8, 4))) * (rng.permutation(8) % 2 * 2.0 - 1.0)[None, :, None]
    u[:, :, ::16] = a.astype(np.float32).astype(BF)
    w = np.zeros((128, 4, 128, 4), np.float32)
    i = np.arange(128)
    for b in range(4): w[i, b, i, b] = -8
    return {"x": x.astype(np.float32).reshape(N, 128, 4 * C).astype(BF), "u": u.reshape(N, 128, 512), "v": d["v"], **common(w.reshape(128, 2048).astype(BF), rng)}
def setup_inputs_spread(rng):
    d = setup_inputs(rng)
    d["x"] = wide(rng, N, 128, 4 * C, cols=6)
    return d
def check_inputs(d):
    b = []
    for k in ("x", "u", "v"):
        a = np.abs(d[k].astype(np.float32))
        if not (np.isfinite(a).all() and ((a == 0) | (a >= 2.0 ** -30) & (a <= 2.0 ** 30)).all()): b.append("a value of " + k)
    if (d["u"].astype(np.float32) != d["u"][:1].astype(np.float32)).any(): b.append("u differs between ranks")
    if (d["wc"] % 128 == 127).any(): b.append("a code of wc is no number")
    if (d["wc"] != d["wc"][:1]).any(): b.append("wc differs between ranks")
    s = [mx_ref.live(p) for p in d["ws"]]
    if any((p != s[0]).any() for p in s): b.append("ws differs between ranks")
    return b
def reference(x, u, v, wc, ws):
    w, qu = pk(wc[0], ws[0]), mx_ref.quantize(u[0])
    now = [x[r] for r in range(N)]
    for t in range(R):
        o = [order(mx_ref.matmul(qu, mx_ref.quantize(now[r]))) for r in range(N)]
        i = [np.argsort(o[r], axis=1) for r in range(N)]
        e = [walk(np.take_along_axis(o[r], i[partner(r, t)], axis=1)) for r in range(N)]
        laid = [gcols(now[r], e[r]) for r in range(N)]
        came = decode(join(*[mx_ref.quantize(np.ascontiguousarray(laid[r][:, :4 * S])) for r in range(N)])).astype(BF)
        for r in range(N):
            z = np.ascontiguousarray(np.concatenate([cut(came, partner(r, t), 4 * S), laid[r][:, 4 * S:]], axis=1))
            q = mx_ref.quantize(z)
            now[r] = tile([z[:, b::4].astype(np.float32) + mx_ref.matmul(pick(w, np.arange(128 * b, 128 * b + 128)), q) * np.float32(0.015625) for b in range(4)])
    y, el = np.zeros((N, 128, C), np.float32), np.zeros((N, 8, C), np.float32)
    oc, osc = np.zeros((N, 128, 4 * C), np.uint8), np.zeros((N, 16, C), np.uint8)
    for r in range(N):
        q = mx_ref.quantize(now[r])
        y[r] = mx_ref.matmul(mx_ref.quantize(v[r]), q)
        el[r] = e[r]
        oc[r], osc[r] = emit(q)
    return {"y": y, "el": el, "oc": oc, "osc": osc}

@@ -1,0 +1,581 @@
+from concourse.mybir import dt, AluOpType as ALU, ActivationFunctionType as ACT
+
+C, S, R = 416, 64, 2
+STEP = [4, 1]
+M = C // 16
+NS = 11
+XD = 4
+NSD = 9
+LO = 2
+H = C // 2
+BIG = float(2 ** 20)
+B16 = 512.0
+KW = 2048.0
+CWT = 64.0
+DBL = 9
+SH = 64
+CUT = 14
+PART = [(16 * CUT, C), (0, 16 * CUT)]
+
+F32, BF, F16, U16, I32, X4, U8 = "float32", "bfloat16", "float16", "uint16", "int32", "float8_e4m3fn_x4", "uint8"
+SCRATCH = {}
+
+
+def _decl(dtype, cols, names, where="sbuf"):
+    for n in names.split():
+        SCRATCH[n] = (where, [128, cols], dtype)
+
+
+_decl(BF, 4 * C, "x0 xn z xp z64 dp")
+_decl(BF, 512, "ut vt ones")
+_decl(BF, 2048, "et")
+_decl(X4, C, "qx0 qx1 qx2 qz0 qz1 lc0 lc1 rc0 rc1")
+_decl(U8, C, "sx0 sx1 sx2 sz0 sz1 ls0 ls1 rs0 rs1")
+_decl(X4, 128, "uq uq2 vq")
+_decl(U8, 128, "us us2 vs")
+_decl(X4, 512, "wq eq")
+_decl(U8, 512, "wp es")
+_decl(U16, 32, "li0 li1 ll0 ll1 rl0 rl1")
+_decl(U16, M, "lm lp le cs lq")
+_decl(U16, M * DBL, "lt")
+_decl(U16, 8, "cu lk le2")
+_decl(F32, C, "p1024 c2 row msk wsc cor ka kb ba bb yy ww elf ybuf")
+_decl(BF, C, "jm dm kp cw ec16 eqf ta tb orow posr erow mrow")
+_decl(F16, C, "ex16")
+_decl(BF, C * (M - NSD), "fl")
+_decl(BF, H * (M - NSD), "res")
+_decl(BF, C * 3, "sfl")
+_decl(BF, 128, "pat")
+_decl(F32, 32, "accl accg t1 t2 cb0 cb1 iw cols pal pag pt1 pt2 pcb")
+_decl(I32, 64, "s32")
+_decl(I32, 8, "pc")
+_decl(I32, 72, "kk ub")
+_decl(F32, S, "nf rr zz z2 ex2 ec ec2 one64")
+_decl(F32, 16 * XD, "prow pmsk pwsc pcor")
+_decl(BF, 16 * XD, "peq")
+_decl(BF, S, "e2r")
+_decl(F32, 512, "psa psb pse psf", "psum")
+_decl(F32, 2048, "psd", "psum")
+
+POOL = {"v": 48, "s": 36, "t": 12, "g": 8}
+SEMAPHORES = [e + str(k) for e in POOL for k in range(POOL[e])]
+SEMAPHORES += ["d%d" % k for k in range(18)]
+SEMAPHORES += ["sent"] + [n + str(t) for t in range(R) for n in ("ac", "al", "hc", "hs", "hl")]
+
+
+def helpers_of(T, topo, r, t):
+    src, dst = T.cores[r], T.cores[r ^ STEP[t]]
+    if topo.may_write(src, dst):
+        return []
+    c = [k for k in topo.cores_of(src) if T.rank_of(k) is None and topo.may_write(k, dst)]
+    c.sort(key=lambda k: topo.die(k) != topo.die(src))
+    return c[:len(PART)]
+
+
+def send(g, T, topo, src, dst, out_ap, in_ap, sem):
+    rid, pid = topo.addr(dst, src)
+    g.remote_dma(out_ap, in_ap, T.sem[sem], T.sem["sent"], pid, rid, topo.mask(src, dst))
+    return len(topo.engines(src, dst))
+
+
+def helper_program(g, core, T, topo):
+    total = 0
+    for t in range(R):
+        for r in range(len(T.cores)):
+            h = helpers_of(T, topo, r, t)
+            if core not in h:
+                continue
+            src, dst = T.cores[r], T.cores[r ^ STEP[t]]
+            n = len(topo.engines(src, core))
+            a, e = PART[h.index(core)]
+            g.wait_ge(T.sem["hc%d" % t], n)
+            total += send(g, T, topo, core, dst, T["lc%d" % t][:, a:e].bitcast(dt.uint8), T["rc%d" % t][:, a:e].bitcast(dt.uint8), "ac%d" % t)
+            g.wait_ge(T.sem["hs%d" % t], n)
+            total += send(g, T, topo, core, dst, T["ls%d" % t][:, a:e], T["rs%d" % t][:, a:e], "ac%d" % t)
+            if core == h[0]:
+                g.wait_ge(T.sem["hl%d" % t], n)
+                total += send(g, T, topo, core, dst, T["ll%d" % t][:, LO:LO + M - XD], T["rl%d" % t][:, LO:LO + M - XD], "al%d" % t)
+    if total:
+        g.wait_ge(T.sem["sent"], total)
+
+
+def rank_program(g, core, T, topo):
+    rank = T.rank_of(core)
+    if rank is None:
+        helper_program(g, core, T, topo)
+        return
+
+    Q = {"v": g.vector, "s": g.scalar, "t": g.tensor, "g": g, "y": g.sync}
+    known = {e: {} for e in Q}
+    count = {}
+    waited = {}
+    last = {}
+    order = []
+    turn = {e: 0 for e in POOL}
+    ndma = [0]
+    nsent = [0]
+    hist = {}
+
+    def wait(e, tok):
+        sem, val, seen = tok
+        if known[e].get(sem, 0) >= val:
+            return
+        Q[e].wait_ge(T.sem[sem], val)
+        waited[sem] = max(waited.get(sem, 0), val)
+        k = known[e]
+        for s2 in seen:
+            if k.get(s2, 0) < seen[s2]:
+                k[s2] = seen[s2]
+        k[sem] = val
+
+    def A(name, a=0, b=None, s=1):
+        n = SCRATCH[name][1][1]
+        b = n if b is None else b
+        m = 0
+        if SCRATCH[name][0] == "psum":
+            m = 1 << (a // 512)
+        elif s == 1:
+            m = ((1 << (b - a)) - 1) << a
+        else:
+            for j in range(a, b, s):
+                m |= 1 << j
+        ap = T[name][:, a:b] if s == 1 else T[name][:, a:b:s]
+        return (ap, [(name, m)])
+
+    def ind(win, off):
+        return (win[0].indirect(off[0]), win[1] + off[1])
+
+    def before(e, reads, writes):
+        need = []
+        for name, m in reads:
+            ps = SCRATCH[name][0] == "psum"
+            for m2, tok, e2, w in hist.get(name, []):
+                if m & m2 and (w or (ps and e2 != e)):
+                    need.append(tok)
+        for name, m in writes:
+            for m2, tok, e2, w in hist.get(name, []):
+                if m & m2:
+                    need.append(tok)
+        need.sort(key=lambda k: -sum(k[2].values()))
+        for tok in need:
+            wait(e, tok)
+
+    def after(e, reads, writes, tok):
+        for name, m in writes:
+            hist[name] = [h for h in hist.get(name, []) if h[0] & ~m] + [(m, tok, e, True)]
+        for name, m in reads:
+            hist.setdefault(name, []).append((m, tok, e, False))
+
+    def regs(xs):
+        out = []
+        for x in xs:
+            if isinstance(x, tuple):
+                out += x[1]
+        return out
+
+    def ap(x):
+        return x[0] if isinstance(x, tuple) else x
+
+    def token(e, sem, n):
+        count[sem] = count.get(sem, 0) + n
+        tok = (sem, count[sem], dict(known[e]))
+        last[sem] = tok
+        order.append(sem)
+        return tok
+
+    def op(e, fn, outs, ins):
+        reads, writes = regs(ins), regs(outs)
+        before(e, reads, writes)
+        sem = e + str(turn[e] % POOL[e])
+        turn[e] += 1
+        if sem in last:
+            wait(e, last[sem])
+        fn().then_inc(T.sem[sem], 1)
+        tok = token(e, sem, 1)
+        after(e, reads, writes, tok)
+        return tok
+
+    def dma(e, out, in_):
+        reads, writes = regs([in_]), regs([out])
+        before(e, reads, writes)
+        sem = "d%d" % ndma[0]
+        ndma[0] += 1
+        Q[e].dma_start(ap(out), ap(in_)).then_inc(T.sem[sem], 16)
+        tok = token(e, sem, 16)
+        after(e, reads, writes, tok)
+        return tok
+
+    def b8(x):
+        return (x[0].bitcast(dt.uint8), x[1])
+
+    def rsend(dst, out, in_, sem):
+        before("g", in_[1], [])
+        nsent[0] += send(g, T, topo, core, dst, out[0], in_[0], sem)
+
+    def arrive(sem, n, parts):
+        count[sem] = n
+        tok = (sem, n, {})
+        last[sem] = tok
+        order.append(sem)
+        after("x", [], regs(parts), tok)
+
+    def cp(o, i):
+        return op("v", lambda: g.vector.tensor_copy(o[0], i[0]), [o], [i])
+
+    def scatter(win, off, i):
+        return op("v", lambda: g.vector.tensor_copy(win[0].indirect(off[0]), i[0]), [win], [i, off])
+
+    def ts(o, i, s1, op0, s2=None, op1=None):
+        if op1 is None:
+            return op("v", lambda: g.vector.tensor_scalar(o[0], i[0], ap(s1), None, op0), [o], [i, s1])
+        return op("v", lambda: g.vector.tensor_scalar(o[0], i[0], ap(s1), ap(s2), op0, op1), [o], [i, s1, s2])
+
+    def tt(o, a, b, f):
+        return op("v", lambda: g.vector.tensor_tensor(o[0], a[0], b[0], f), [o], [a, b])
+
+    def scan(o, a, b, init, f0, f1):
+        return op("v", lambda: g.vector.tensor_tensor_scan(o[0], a[0], b[0], init, f0, f1), [o], [a, b])
+
+    def mset(o, v):
+        return op("v", lambda: g.vector.memset(o[0], v), [o], [])
+
+    def quant(q, s, i):
+        return op("v", lambda: g.vector.quantize_mx(q[0], s[0], i[0]), [q, s], [i])
+
+    def act(o, i, f, scale=1.0, bias=None, acc=None):
+        kw = {"scale": ap(scale)}
+        if bias is not None:
+            kw["bias"] = ap(bias)
+        if acc is not None:
+            kw["accum_out"] = acc[0]
+        return op("s", lambda: g.scalar.activation(o[0], i[0], f, **kw), [o, acc], [i, scale, bias])
+
+    def mm(o, w, ws, x, xs):
+        return op("t", lambda: g.tensor.matmul_mx(o[0], w[0], ws[0], x[0], xs[0], True, True), [o], [w, ws, x, xs])
+
+    QC, QM1, Q63, OFF, OFF16 = [A("cols", k, k + 1) for k in range(5)]
+
+    def scan16(rowv, n=C):
+        scan(A("ex16", 0, n), rowv, A("ec16", 0, n), -B16, ALU.max, ALU.add)
+
+    def list16(lst, n=C):
+        ts(lst, A("ex16", 15, n, 16), OFF16, ALU.subtract)
+
+    def ship(t, h):
+        mine = helpers_of(T, topo, rank, t)
+        if mine:
+            a, e = PART[h]
+            rsend(mine[h], b8(A("rc%d" % t, a, e)), b8(A("qx%d" % t, a, e)), "hc%d" % t)
+            rsend(mine[h], A("rs%d" % t, a, e), A("sx%d" % t, a, e), "hs%d" % t)
+        elif h == len(PART) - 1:
+            rsend(T.cores[rank ^ STEP[t]], b8(A("lc%d" % t)), b8(A("qx%d" % t)), "ac%d" % t)
+            rsend(T.cores[rank ^ STEP[t]], A("ls%d" % t), A("sx%d" % t), "ac%d" % t)
+
+    nss = [NSD if helpers_of(T, topo, rank, t) else NS for t in range(R)]
+
+    dma("y", A("ut"), T.u[:])
+    tx1 = dma("s", A("x0", 2 * C, 4 * C), T.x[:, 2 * C:4 * C])
+    tx0 = dma("y", A("x0", 0, 2 * C), T.x[:, 0:2 * C])
+    wait("y", tx0)
+    wait("y", tx1)
+    dma("y", A("vt"), T.v[:])
+    dma("y", b8(A("wq")), T.wc[:])
+    dma("y", A("wp"), T.ws[:])
+
+    op("g", lambda: g.iota(T.pc[:, 0:2], [[-1, 2]], 16, 1), [A("pc", 0, 2)], [])
+    op("g", lambda: g.iota(T.s32[:], [[1, 64]], 0, 0), [A("s32")], [])
+    op("g", lambda: g.iota(T.jm[:], [[1, C]], -H, 0, allow_small_or_imprecise_dtypes=True), [A("jm")], [])
+    mset(A("accl", 0, 1), 0.0)
+    mset(A("ub", 0, 1), 1)
+    ts(A("pc", 2, 4), A("pc", 0, 2), 15, ALU.bitwise_and)
+    mset(A("one64"), 1.0)
+    cp(A("cols", 0, 2), A("pc", 2, 4))
+    r16 = A("s32", 0, 16)
+    ts(A("pat", 16, 32), r16, 0.0, ALU.not_equal)
+    ts(A("pat", 0, 16), r16, QC, ALU.is_equal)
+    ts(A("lq"), A("s32", 0, M), 0.0, ALU.mult, QC, ALU.add)
+    ts(Q63, QC, 0.0, ALU.is_gt, CWT - 1.0, ALU.mult)
+    ts(A("cols", 5, 6), QC, 0.0, ALU.is_gt, 2.0, ALU.mult)
+    act(A("dm"), ind(A("pat", 0, 16), A("lq")), ACT.Copy)
+    act(A("kp"), ind(A("pat", 16, 32), A("lq")), ACT.Copy)
+    ts(A("pat", 80, 96), r16, QC, ALU.is_equal, Q63, ALU.mult)
+    ts(A("pat", 96, 112), r16, QM1, ALU.is_equal, -2.0, ALU.mult)
+    ts(A("cu"), A("s32", 0, 8), 16.0, ALU.mult)
+    tt(A("pat", 32, 48), A("pat", 80, 96), A("pat", 16, 32), ALU.add)
+    tt(A("pat", 48, 64), A("pat", 96, 112), A("pat", 0, 16), ALU.add)
+    act(A("cw"), ind(A("pat", 32, 48), A("lq")), ACT.Copy)
+    act(A("ec16"), ind(A("pat", 48, 64), A("lq")), ACT.Copy, scale=B16)
+    ts(A("cs"), A("s32", 0, M), 16.0, ALU.mult, 15.0, ALU.add)
+    for t in range(R):
+        ts(A("cb%d" % t, 0, nss[t]), A("s32", 0, nss[t]), 16.0, ALU.mult)
+        mset(A("cb%d" % t, nss[t], M), float(H))
+    ts(A("pcb", 0, XD), A("s32", M - XD, M), 16.0, ALU.mult)
+    ts(OFF, A("cols", 5, 6), 1.0, ALU.subtract, BIG, ALU.mult)
+    ts(OFF16, A("cols", 5, 6), B16, ALU.mult, B16 + H, ALU.subtract)
+    mset(A("ones"), 1.0)
+    tt(A("zz"), A("s32"), A("dm", 0, S), ALU.mult)
+    quant(A("uq"), A("us"), A("ut"))
+    op("v", lambda: g.vector.tensor_copy(T.uq2[:, 0:128].bitcast(dt.uint32), T.uq[:, 0:128].bitcast(dt.uint32).indirect(T.cu[:, 0:8])),
+       [A("uq2")], [A("uq"), A("cu")])
+    op("s", lambda: g.scalar.activation(T.us2[:, 0:128], T.us[:, 0:128].indirect(T.cu[:, 0:8]), ACT.Copy), [A("us2")], [A("us"), A("cu")])
+    quant(A("qx0", H, C), A("sx0", H, C), A("x0", 2 * C, 4 * C))
+    quant(A("qx0", 0, H), A("sx0", 0, H), A("x0", 0, 2 * C))
+    for h in range(len(PART)):
+        ship(0, h)
+
+    for t in range(R):
+        partner = T.cores[rank ^ STEP[t]]
+        mine = helpers_of(T, topo, rank, t)
+        theirs = helpers_of(T, topo, rank ^ STEP[t], t)
+        qx, sx = "qx%d" % t, "sx%d" % t
+        li, ll, lc, ls = "li%d" % t, "ll%d" % t, "lc%d" % t, "ls%d" % t
+        qz, sz = "qz%d" % t, "sz%d" % t
+        ns, cb = nss[t], "cb%d" % t
+        me = M - XD if mine else M
+
+        mm(A("psa", 0, C), A("uq2"), A("us2"), A(qx), A(sx))
+        mm(A("psb", 0, C), A("uq2"), A("us2"), A(qx), A(sx))
+        srcs = theirs if theirs else [partner]
+        arrive("ac%d" % t, sum(2 * len(topo.engines(k, core)) for k in srcs), [A(lc), A(ls)])
+        arrive("al%d" % t, len(topo.engines(srcs[0], core)), [A(ll, LO, LO + me)])
+        if t == 0:
+            for b in range(4):
+                op("g", lambda: g.affine_select(T.et[:, 512 * b:512 * b + 512], T.ones[:], [[-1, 512]], ALU.is_equal, 0.0, b, 4),
+                   [A("et", 512 * b, 512 * b + 512)], [A("ones")])
+
+        cut = 16 * ns
+        tt(A("msk", 0, cut), A("psa", 0, cut), A("dm", 0, cut), ALU.mult)
+        act(A("row"), A("psb", 0, C), ACT.Copy)
+        scan(A("wsc", 0, cut), A("kp", 0, cut), A("msk", 0, cut), 0.0, ALU.mult, ALU.add)
+        tt(A("msk", cut, C), A("psa", cut, C), A("dm", cut, C), ALU.mult)
+        scan(A("wsc", cut, C), A("kp", cut, C), A("msk", cut, C), 0.0, ALU.mult, ALU.add)
+
+        def s_blocks(blocks, bank, w, accl, accg):
+            def first(k):
+                o = (k % 3) * C
+                act(A("sfl", o, o + C), A(bank, 0, C), ACT.Sign, scale=-1.0, bias=A(w, 16 * k + 15, 16 * k + 16))
+
+            first(0)
+            for k, m in enumerate(blocks):
+                if k + 1 < len(blocks):
+                    first(k + 1)
+                o = (k % 3) * C
+                if m:
+                    act(A("sfl", o, o + 16 * m), A("sfl", o, o + 16 * m), ACT.Relu, acc=A(accl, k, k + 1))
+                act(A("sfl", o + 16 * m, o + C), A("sfl", o + 16 * m, o + C), ACT.Relu, scale=-1.0, acc=A(accg, k, k + 1))
+
+        def v_first(m):
+            o, w = (m - ns) * C, A("wsc", 16 * m + 15, 16 * m + 16)
+            ts(A("fl", o, o + 16 * m), A("psa", 0, 16 * m), w, ALU.is_ge)
+            ts(A("fl", o + 16 * m, o + C), A("psa", 16 * m, C), w, ALU.is_gt)
+
+        def v_second(m):
+            o, k = (m - ns) * C, (m - ns) * H
+            scan(A("res", k, k + H), A("fl", o, o + H), A("fl", o + H, o + C), -float(H), ALU.add, ALU.add)
+
+        def v_sum(m0, m1):
+            tt(A("iw", m0, m1), A("t2", m0, m1), A("res", H * (m0 - ns) + H - 1, H * (m1 - ns), H), ALU.add)
+
+        s_blocks(list(range(ns)), "psb", "wsc", "accl", "accg")
+        tt(A("eqf"), ind(A("wsc"), A("cs")), A("row"), ALU.is_equal)
+        v_first(ns)
+        scan(A("cor"), A("cw"), A("eqf"), 0.0, ALU.mult, ALU.add)
+        for m in range(ns, me):
+            if m + 1 < me:
+                v_first(m + 1)
+            if m == ns:
+                ts(A("t1", 0, M), A("cor", 15, C, 16), 1.0 / CWT, ALU.mult)
+            if m == ns + 1:
+                tt(A("t2", 0, M), A("t1", 0, M), A(cb, 0, M), ALU.add)
+            v_second(m)
+        tt(A("t1", 0, ns), A("t2", 0, ns), A("accl", 0, ns), ALU.subtract)
+        v_sum(ns, me)
+        tt(A("iw", 0, ns), A("t1", 0, ns), A("accg", 0, ns), ALU.add)
+        cp(A(li, LO, LO + me), A("iw", 0, me))
+        if mine:
+            rsend(mine[0], A("rl%d" % t, LO, LO + me), A(li, LO, LO + me), "hl%d" % t)
+        else:
+            rsend(partner, A(ll, LO, LO + me), A(li, LO, LO + me), "al%d" % t)
+
+        if mine:
+            n = 16 * XD
+            mm(A("psf", 0, 128), A("uq2"), A("us2"), A(lc, C - 128, C), A(ls, C - 128, C))
+            mm(A("pse", 0, C), A("uq2"), A("us2"), A(lc), A(ls))
+            tt(A("pmsk"), A("psf", 128 - n, 128), A("dm", 0, n), ALU.mult)
+            act(A("prow"), A("pse", C - n, C), ACT.Copy)
+            v_first(me)
+            scan(A("pwsc"), A("kp", 0, n), A("pmsk"), 0.0, ALU.mult, ALU.add)
+            s_blocks(list(range(me, M)), "pse", "pwsc", "pal", "pag")
+            for m in range(me, M):
+                if m + 1 < M:
+                    v_first(m + 1)
+                if m == me:
+                    tt(A("peq"), ind(A("pwsc"), A("cs", 0, XD)), A("prow"), ALU.is_equal)
+                if m == me + 1:
+                    scan(A("pcor"), A("cw", 0, n), A("peq"), 0.0, ALU.mult, ALU.add)
+                if m == me + 2:
+                    ts(A("pt1", 0, XD), A("pcor", 15, n, 16), 1.0 / CWT, ALU.mult)
+                if m == me + 3:
+                    tt(A("pt2", 0, XD), A("pt1", 0, XD), A("pcb", 0, XD), ALU.add)
+                v_second(m)
+            v_sum(me, M)
+            cp(A(li, LO + me, LO + M), A("iw", me, M))
+        scatter(A("orow"), A(li, LO, LO + M), A("jm"))
+        if mine:
+            tt(A("pt1", 0, XD), A("pt2", 0, XD), A("pal", 0, XD), ALU.subtract)
+            tt(A("pt2", 0, XD), A("pt1", 0, XD), A("pag", 0, XD), ALU.add)
+            cp(A(ll, LO + me, LO + M), A("pt2", 0, XD))
+        if t == 0:
+            act(A("p1024"), A("jm"), ACT.Identity, scale=KW, bias=KW * H)
+            act(A("c2"), A("jm"), ACT.Identity, scale=KW, bias=KW * (H - 1))
+            act(A("ec"), A("ec16", 0, S), ACT.Copy, scale=BIG / B16)
+            quant(A("eq"), A("es"), A("et"))
+            quant(A("vq"), A("vs"), A("vt"))
+        for b in range(4):
+            mm(A("psd", 512 * b, 512 * b + C), A("eq", 128 * b, 128 * b + 128), A("es", 128 * b, 128 * b + 128), A(lc), A(ls))
+
+        tb_, kb_, bb_ = ["ta", "tb"], ["ka", "kb"], ["ba", "bb"]
+        act(A("ta"), ind(A("orow"), A(ll, LO, LO + M)), ACT.Copy)
+        ts(A("ka"), ind(A("orow"), A(ll, LO, LO + M)), KW, ALU.mult, KW * H + 1.0, ALU.add)
+        act(A("ba"), A("ta"), ACT.Identity, scale=KW, bias=KW * H + 2.0)
+        scan16(A("ta"))
+        list16(A("lt", 0, M))
+        for k in range(DBL):
+            L = A("lt", k * M, k * M + M)
+            a, b = k % 2, (k + 1) % 2
+            if k + 1 < DBL:
+                act(A(tb_[b]), ind(A(tb_[a]), L), ACT.Copy)
+            tt(A(kb_[b]), ind(A(bb_[a]), L), A(kb_[a]), ALU.min)
+            if k + 1 < DBL:
+                n = float(2 ** (k + 1))
+                act(A(bb_[b], SH, C), A(kb_[b], SH, C), ACT.Identity, bias=n)
+                scan16(A(tb_[b]))
+                ts(A(bb_[b], 0, SH), A(kb_[b], 0, SH), n, ALU.add)
+                list16(A("lt", (k + 1) * M, (k + 2) * M))
+        K = A(kb_[DBL % 2])
+
+        def unpack(b):
+            act(A("dp", b * C, b * C + C), A("psd", 512 * b, 512 * b + C), ACT.Copy)
+
+        unpack(0)
+        act(A("mrow"), K, ACT.Identity, scale=1.0 / KW, bias=-float(H))
+        for b in range(1, 4):
+            unpack(b)
+        if t == 0:
+            for b in range(4):
+                act(A("xp", b * C, b * C + C), A("x0", b, 4 * C, 4), ACT.Copy, scale=64.0)
+        scan(A("yy"), K, A("p1024"), 0.0, ALU.max, ALU.max)
+        scan16(A("mrow"))
+        scan(A("ww"), A("yy"), A("c2"), -KW - H, ALU.add, ALU.subtract)
+        list16(A("lm"))
+        tt(A("posr"), ind(A("ww"), A("lm")), K, ALU.subtract)
+        scan16(A("posr"))
+        if t == 0:
+            tt(A("ec2"), A("zz"), A("ec"), ALU.add)
+        list16(A("lp"))
+        scatter(A("erow"), A("lp"), A("jm"))
+        scan16(A("erow"))
+        list16(A("le"))
+
+        banks = [[A("psd", 512 * b, 512 * b + PART[0][1] - PART[0][0]) for b in range(4)],
+                 [A(n, 0, PART[1][1]) for n in ("psa", "psb", "pse", "psf")]]
+        nx, ns_ = "qx%d" % (t + 1), "sx%d" % (t + 1)
+
+        def tile(name, h, b):
+            return A(name, 4 * PART[h][0] + b, 4 * PART[h][1], 4)
+
+        def plane(name, h, b):
+            return A(name, b * C + PART[h][0], b * C + PART[h][1])
+
+        def layer(h):
+            a, e = PART[h]
+            quant(A(qz, a, e), A(sz, a, e), A("z", 4 * a, 4 * e))
+            for b in range(4):
+                mm(banks[h][b], A("wq", 128 * b, 128 * b + 128), A("wp", 128 * b, 128 * b + 128), A(qz, a, e), A(sz, a, e))
+
+        def finish(h):
+            a, e = PART[h]
+            quant(A(nx, a, e), A(ns_, a, e), A("xn", 4 * a, 4 * e))
+            if t == R - 1:
+                mm(A("psd", 512 * h, 512 * h + e - a), A("vq"), A("vs"), A(nx, a, e), A(ns_, a, e))
+                dma("y", T.oc[:, 4 * a:4 * e], b8(A(nx, a, e)))
+            else:
+                ship(t + 1, h)
+
+        def up_v(h, b):
+            ts(plane("z64", h, b), tile("z", h, b), 64.0, ALU.mult)
+
+        def down_v(h, b):
+            ts(tile("xn", h, b), plane("xp", h, b), 1.0 / 64.0, ALU.mult)
+
+        def down_s(h, b):
+            act(tile("xn", h, b), plane("xp", h, b), ACT.Copy, scale=1.0 / 64.0)
+
+        def add(h, b):
+            tt(plane("xp", h, b), banks[h][b], plane("z64", h, b), ALU.add)
+
+        for b in range(4):
+            act(tile("z", 0, b), ind(A("xp", b * C, b * C + C), A("le", CUT, M)), ACT.Copy, scale=1.0 / 64.0)
+        for b in range(4):
+            act(A("z", 4 * S + b, 64 * CUT, 4), ind(A("xp", b * C, b * C + C), A("le", 4, CUT)), ACT.Copy, scale=1.0 / 64.0)
+        cp(A("kk", 0, S), ind(K, A("le", 0, 4)))
+        ts(A("ub", 1, S + 1), A("kk", 0, S), int(KW) - 1, ALU.bitwise_and)
+        ts(A("nf"), A("ub", 0, S), 1.0, ALU.not_equal)
+        scan(A("rr"), A("one64"), A("nf"), 0.0, ALU.add, ALU.mult)
+        tt(A("zz"), A("ub", 1, S + 1), A("rr"), ALU.subtract)
+        tt(A("z2"), A("zz"), A("nf"), ALU.mult)
+        scan(A("ex2"), A("z2"), A("ec2"), -BIG, ALU.max, ALU.add)
+        up_v(0, 0)
+        ts(A("lk", 0, 4), A("ex2", 15, S, 16), OFF, ALU.subtract)
+        up_v(0, 1)
+        cp(A("e2r"), ind(A("erow"), A("lk", 0, 4)))
+        up_v(0, 2)
+        scan16(A("e2r"), S)
+        layer(0)
+        list16(A("le2", 0, 4), S)
+        up_v(0, 3)
+        for b in range(4):
+            cp(A("z", b, 4 * S, 4), ind(A("dp", b * C, b * C + C), A("le2", 0, 4)))
+        layer(1)
+        for b in range(4):
+            act(plane("z64", 1, b), tile("z", 1, b), ACT.Copy, scale=64.0)
+        for b in range(4):
+            add(0, b)
+        down_s(0, 0)
+        down_s(0, 1)
+        down_v(0, 2)
+        down_v(0, 3)
+        add(1, 0)
+        down_s(1, 0)
+        finish(0)
+        add(1, 1)
+        down_s(1, 1)
+        add(1, 2)
+        down_s(1, 2)
+        add(1, 3)
+        down_v(1, 3)
+        if t == R - 1:
+            a, e = PART[0]
+            act(A("ybuf", a, e), A("psd", 0, e - a), ACT.Copy)
+            dma("s", T.y[:, a:e], A("ybuf", a, e))
+        finish(1)
+
+    a, e = PART[1]
+    cp(A("ybuf", a, e), A("psd", 512, 512 + e))
+    act(A("elf"), A("erow"), ACT.Identity, bias=float(H))
+    dma("y", T.y[:, a:e], A("ybuf", a, e))
+    dma("s", T.el[:], (T.elf[0:128:16, :], A("elf")[1]))
+    sx = "sx%d" % R
+    for k in range(4):
+        dma("s", T.osc[4 * k:4 * k + 4, :], (T[sx][32 * k:32 * k + 4, :], A(sx)[1]))
+
+    g.wait_ge(T.sem["sent"], nsent[0])
+    done = set()
+    ends = []
+    for sem in reversed(order):
+        if sem not in done:
+            done.add(sem)
+            ends.append(sem)
+    for sem in reversed(ends):
+        if waited.get(sem, 0) < count[sem]:
+            g.wait_ge(T.sem[sem], count[sem])

@@ -13,7 +13,8 @@ B16 = 512.0
 KW = 2048.0
 CWT = 64.0
 DBL = 9
-SH = 64
+MA = 14
+HA = 16 * MA
 CUT = 14
 PART = [(16 * CUT, C), (0, 16 * CUT)]
 
@@ -38,22 +39,24 @@ _decl(U8, 512, "wp es")
 _decl(U16, 32, "li0 li1 ll0 ll1 rl0 rl1")
 _decl(U16, M, "lm lp le cs lq")
 _decl(U16, M * DBL, "lt")
-_decl(U16, 8, "cu lk le2")
+_decl(U16, 8, "cu lk le2 le3 lcc")
 _decl(F32, C, "p1024 c2 row msk wsc cor ka kb ba bb yy ww elf ybuf")
-_decl(BF, C, "jm dm kp cw ec16 eqf ta tb orow posr erow mrow")
+_decl(BF, C, "jm dm kp cw ec16 eqf ta tb tp orow posr erow mrow")
 _decl(F16, C, "ex16")
+_decl(F16, S, "ex17")
 _decl(BF, C * (M - NSD), "fl")
 _decl(BF, H * (M - NSD), "res")
 _decl(BF, C * 3, "sfl")
 _decl(BF, 128, "pat")
-_decl(F32, 32, "accl accg t1 t2 cb0 cb1 iw cols pal pag pt1 pt2 pcb")
+_decl(F32, 32, "accl accg t1 t2 cb0 cb1 iw cols pal pag pt1 pt2 pcb kc cc")
 _decl(I32, 64, "s32")
 _decl(I32, 8, "pc")
-_decl(I32, 72, "kk ub")
-_decl(F32, S, "nf rr zz z2 ex2 ec ec2 one64")
+_decl(F32, 72, "endb")
+_decl(F32, S, "zz se seg ex2 ec ec2")
+_decl(F32, 4 * S, "sj")
 _decl(F32, 16 * XD, "prow pmsk pwsc pcor")
 _decl(BF, 16 * XD, "peq")
-_decl(BF, S, "e2r")
+_decl(BF, S, "e2r e3r")
 _decl(F32, 512, "psa psb pse psf", "psum")
 _decl(F32, 2048, "psd", "psum")
 
@@ -255,11 +258,11 @@ def rank_program(g, core, T, topo):
 
     QC, QM1, Q63, OFF, OFF16 = [A("cols", k, k + 1) for k in range(5)]
 
-    def scan16(rowv, n=C):
-        scan(A("ex16", 0, n), rowv, A("ec16", 0, n), -B16, ALU.max, ALU.add)
+    def scan16(rowv, a=0, e=C, buf="ex16"):
+        scan(A(buf, a, e), rowv, A("ec16", a, e), -B16, ALU.max, ALU.add)
 
-    def list16(lst, n=C):
-        ts(lst, A("ex16", 15, n, 16), OFF16, ALU.subtract)
+    def list16(lst, a=0, e=C, buf="ex16"):
+        ts(lst, A(buf, a + 15, e, 16), OFF16, ALU.subtract)
 
     def ship(t, h):
         mine = helpers_of(T, topo, rank, t)
@@ -286,9 +289,8 @@ def rank_program(g, core, T, topo):
     op("g", lambda: g.iota(T.s32[:], [[1, 64]], 0, 0), [A("s32")], [])
     op("g", lambda: g.iota(T.jm[:], [[1, C]], -H, 0, allow_small_or_imprecise_dtypes=True), [A("jm")], [])
     mset(A("accl", 0, 1), 0.0)
-    mset(A("ub", 0, 1), 1)
+    mset(A("endb", 0, 1), -1.0)
     ts(A("pc", 2, 4), A("pc", 0, 2), 15, ALU.bitwise_and)
-    mset(A("one64"), 1.0)
     cp(A("cols", 0, 2), A("pc", 2, 4))
     r16 = A("s32", 0, 16)
     ts(A("pat", 16, 32), r16, 0.0, ALU.not_equal)
@@ -312,7 +314,9 @@ def rank_program(g, core, T, topo):
     ts(A("pcb", 0, XD), A("s32", M - XD, M), 16.0, ALU.mult)
     ts(OFF, A("cols", 5, 6), 1.0, ALU.subtract, BIG, ALU.mult)
     ts(OFF16, A("cols", 5, 6), B16, ALU.mult, B16 + H, ALU.subtract)
+    ts(A("kc", 4, 8), A("s32", 0, 4), 16.0, ALU.mult, QC, ALU.add)
     mset(A("ones"), 1.0)
+    ts(A("kc", 0, 4), A("kc", 4, 8), 0.5, ALU.subtract)
     tt(A("zz"), A("s32"), A("dm", 0, S), ALU.mult)
     quant(A("uq"), A("us"), A("ut"))
     op("v", lambda: g.vector.tensor_copy(T.uq2[:, 0:128].bitcast(dt.uint32), T.uq[:, 0:128].bitcast(dt.uint32).indirect(T.cu[:, 0:8])),
@@ -346,8 +350,8 @@ def rank_program(g, core, T, topo):
         cut = 16 * ns
         tt(A("msk", 0, cut), A("psa", 0, cut), A("dm", 0, cut), ALU.mult)
         act(A("row"), A("psb", 0, C), ACT.Copy)
-        scan(A("wsc", 0, cut), A("kp", 0, cut), A("msk", 0, cut), 0.0, ALU.mult, ALU.add)
         tt(A("msk", cut, C), A("psa", cut, C), A("dm", cut, C), ALU.mult)
+        scan(A("wsc", 0, cut), A("kp", 0, cut), A("msk", 0, cut), 0.0, ALU.mult, ALU.add)
         scan(A("wsc", cut, C), A("kp", cut, C), A("msk", cut, C), 0.0, ALU.mult, ALU.add)
 
         def s_blocks(blocks, bank, w, accl, accg):
@@ -403,8 +407,8 @@ def rank_program(g, core, T, topo):
             mm(A("pse", 0, C), A("uq2"), A("us2"), A(lc), A(ls))
             tt(A("pmsk"), A("psf", 128 - n, 128), A("dm", 0, n), ALU.mult)
             act(A("prow"), A("pse", C - n, C), ACT.Copy)
-            v_first(me)
             scan(A("pwsc"), A("kp", 0, n), A("pmsk"), 0.0, ALU.mult, ALU.add)
+            v_first(me)
             s_blocks(list(range(me, M)), "pse", "pwsc", "pal", "pag")
             for m in range(me, M):
                 if m + 1 < M:
@@ -429,29 +433,34 @@ def rank_program(g, core, T, topo):
             act(A("p1024"), A("jm"), ACT.Identity, scale=KW, bias=KW * H)
             act(A("c2"), A("jm"), ACT.Identity, scale=KW, bias=KW * (H - 1))
             act(A("ec"), A("ec16", 0, S), ACT.Copy, scale=BIG / B16)
+            for b in range(2):
+                act(A("xp", b * C, b * C + C), A("x0", b, 4 * C, 4), ACT.Copy, scale=64.0)
             quant(A("eq"), A("es"), A("et"))
-            quant(A("vq"), A("vs"), A("vt"))
         for b in range(4):
             mm(A("psd", 512 * b, 512 * b + C), A("eq", 128 * b, 128 * b + 128), A("es", 128 * b, 128 * b + 128), A(lc), A(ls))
 
         tb_, kb_, bb_ = ["ta", "tb"], ["ka", "kb"], ["ba", "bb"]
-        act(A("ta"), ind(A("orow"), A(ll, LO, LO + M)), ACT.Copy)
+        act(A("tp"), ind(A("orow"), A(ll, LO, LO + M)), ACT.Copy)
         ts(A("ka"), ind(A("orow"), A(ll, LO, LO + M)), KW, ALU.mult, KW * H + 1.0, ALU.add)
-        act(A("ba"), A("ta"), ACT.Identity, scale=KW, bias=KW * H + 2.0)
-        scan16(A("ta"))
+        act(A("ba"), A("tp"), ACT.Identity, scale=KW, bias=KW * H + 2.0)
+        scan16(A("tp"))
         list16(A("lt", 0, M))
+        halves = [(0, MA), (MA, M)]
         for k in range(DBL):
-            L = A("lt", k * M, k * M + M)
             a, b = k % 2, (k + 1) % 2
-            if k + 1 < DBL:
-                act(A(tb_[b]), ind(A(tb_[a]), L), ACT.Copy)
-            tt(A(kb_[b]), ind(A(bb_[a]), L), A(kb_[a]), ALU.min)
-            if k + 1 < DBL:
-                n = float(2 ** (k + 1))
-                act(A(bb_[b], SH, C), A(kb_[b], SH, C), ACT.Identity, bias=n)
-                scan16(A(tb_[b]))
-                ts(A(bb_[b], 0, SH), A(kb_[b], 0, SH), n, ALU.add)
-                list16(A("lt", (k + 1) * M, (k + 2) * M))
+            if k + 1 == DBL:
+                tt(A(kb_[b]), ind(A(bb_[a]), A("lt", k * M, k * M + M)), A(kb_[a]), ALU.min)
+                break
+            for c, e in halves:
+                act(A(tb_[b], 16 * c, 16 * e), ind(A(tb_[a] if k else "tp"), A("lt", k * M + c, k * M + e)), ACT.Copy)
+            for c, e in halves:
+                tt(A(kb_[b], 16 * c, 16 * e), ind(A(bb_[a]), A("lt", k * M + c, k * M + e)), A(kb_[a], 16 * c, 16 * e), ALU.min)
+            for c, e in halves:
+                scan16(A(tb_[b], 16 * c, 16 * e), 16 * c, 16 * e)
+            for c, e in halves:
+                list16(A("lt", (k + 1) * M + c, (k + 1) * M + e), 16 * c, 16 * e)
+            for c, e in halves:
+                act(A(bb_[b], 16 * c, 16 * e), A(kb_[b], 16 * c, 16 * e), ACT.Identity, bias=float(2 ** (k + 1)))
         K = A(kb_[DBL % 2])
 
         def unpack(b):
@@ -459,23 +468,36 @@ def rank_program(g, core, T, topo):
 
         unpack(0)
         act(A("mrow"), K, ACT.Identity, scale=1.0 / KW, bias=-float(H))
-        for b in range(1, 4):
-            unpack(b)
-        if t == 0:
-            for b in range(4):
-                act(A("xp", b * C, b * C + C), A("x0", b, 4 * C, 4), ACT.Copy, scale=64.0)
+        unpack(1)
+        unpack(2)
         scan(A("yy"), K, A("p1024"), 0.0, ALU.max, ALU.max)
-        scan16(A("mrow"))
-        scan(A("ww"), A("yy"), A("c2"), -KW - H, ALU.add, ALU.subtract)
-        list16(A("lm"))
-        tt(A("posr"), ind(A("ww"), A("lm")), K, ALU.subtract)
-        scan16(A("posr"))
         if t == 0:
-            tt(A("ec2"), A("zz"), A("ec"), ALU.add)
+            tt(A("ec2"), A("ec"), A("zz"), ALU.subtract)
+        else:
+            quant(A("vq"), A("vs"), A("vt"))
+        scan(A("ww"), A("yy"), A("c2"), -KW - H, ALU.add, ALU.subtract)
+        scan16(A("mrow"))
+        scan(A("endb", 1, S + 1), A("yy", 0, S), A("p1024", 0, S), -1.0, ALU.add, ALU.subtract)
+        list16(A("lm"))
+        for m in range(4):
+            act(A("sj", S * m, S * m + S), A("endb", 1, S + 1), ACT.Sign, scale=-1.0, bias=A("kc", m, m + 1), acc=A("cc", m, m + 1))
+        unpack(3)
+        tt(A("se"), A("endb", 0, S), A("endb", 1, S + 1), ALU.add)
+        tt(A("posr"), ind(A("ww"), A("lm")), K, ALU.subtract)
+        ts(A("lcc", 0, 4), A("cc", 0, 4), float(S), ALU.add, 0.5, ALU.mult)
+        scan16(A("posr"))
+        act(A("seg"), ind(A("se"), A("lcc", 0, 4)), ACT.Identity, bias=1.0)
+        if t == 0:
+            for b in range(2, 4):
+                act(A("xp", b * C, b * C + C), A("x0", b, 4 * C, 4), ACT.Copy, scale=64.0)
         list16(A("lp"))
+        scan(A("ex2"), A("seg"), A("ec2"), -BIG, ALU.max, ALU.add)
         scatter(A("erow"), A("lp"), A("jm"))
+        ts(A("lk", 0, 4), A("ex2", 15, S, 16), OFF, ALU.subtract)
         scan16(A("erow"))
+        cp(A("e2r"), ind(A("erow"), A("lk", 0, 4)))
         list16(A("le"))
+        scan16(A("e2r"), 0, S, "ex17")
 
         banks = [[A("psd", 512 * b, 512 * b + PART[0][1] - PART[0][0]) for b in range(4)],
                  [A(n, 0, PART[1][1]) for n in ("psa", "psb", "pse", "psf")]]
@@ -514,33 +536,35 @@ def rank_program(g, core, T, topo):
         def add(h, b):
             tt(plane("xp", h, b), banks[h][b], plane("z64", h, b), ALU.add)
 
+        def own_v(b, c0, c1):
+            ts(A("z", 64 * c0 + b, 64 * c1, 4), ind(A("xp", b * C, b * C + C), A("le", c0, c1)), 1.0 / 64.0, ALU.mult)
+
+        def own_s(b, c0, c1):
+            act(A("z", 64 * c0 + b, 64 * c1, 4), ind(A("xp", b * C, b * C + C), A("le", c0, c1)), ACT.Copy, scale=1.0 / 64.0)
+
+        for b in range(3):
+            own_s(b, CUT, M)
         for b in range(4):
-            act(tile("z", 0, b), ind(A("xp", b * C, b * C + C), A("le", CUT, M)), ACT.Copy, scale=1.0 / 64.0)
-        for b in range(4):
-            act(A("z", 4 * S + b, 64 * CUT, 4), ind(A("xp", b * C, b * C + C), A("le", 4, CUT)), ACT.Copy, scale=1.0 / 64.0)
-        cp(A("kk", 0, S), ind(K, A("le", 0, 4)))
-        ts(A("ub", 1, S + 1), A("kk", 0, S), int(KW) - 1, ALU.bitwise_and)
-        ts(A("nf"), A("ub", 0, S), 1.0, ALU.not_equal)
-        scan(A("rr"), A("one64"), A("nf"), 0.0, ALU.add, ALU.mult)
-        tt(A("zz"), A("ub", 1, S + 1), A("rr"), ALU.subtract)
-        tt(A("z2"), A("zz"), A("nf"), ALU.mult)
-        scan(A("ex2"), A("z2"), A("ec2"), -BIG, ALU.max, ALU.add)
-        up_v(0, 0)
-        ts(A("lk", 0, 4), A("ex2", 15, S, 16), OFF, ALU.subtract)
-        up_v(0, 1)
-        cp(A("e2r"), ind(A("erow"), A("lk", 0, 4)))
-        up_v(0, 2)
-        scan16(A("e2r"), S)
-        layer(0)
-        list16(A("le2", 0, 4), S)
+            own_s(b, 4, CUT)
+        list16(A("le2", 0, 4), 0, S, "ex17")
+        own_v(3, CUT, M)
+        cp(A("e3r"), ind(A("tp"), A("le2", 0, 4)))
         up_v(0, 3)
+        scan16(A("e3r"), 0, S, "ex17")
+        up_v(0, 0)
+        list16(A("le3", 0, 4), 0, S, "ex17")
+        layer(0)
         for b in range(4):
-            cp(A("z", b, 4 * S, 4), ind(A("dp", b * C, b * C + C), A("le2", 0, 4)))
+            cp(A("z", b, 4 * S, 4), ind(A("dp", b * C, b * C + C), A("le3", 0, 4)))
+        up_v(0, 1)
+        up_v(0, 2)
+        add(0, 0)
+        add(0, 1)
         layer(1)
         for b in range(4):
             act(plane("z64", 1, b), tile("z", 1, b), ACT.Copy, scale=64.0)
-        for b in range(4):
-            add(0, b)
+        add(0, 2)
+        add(0, 3)
         down_s(0, 0)
         down_s(0, 1)
         down_v(0, 2)

@@ -3,20 +3,21 @@ from concourse.mybir import dt, AluOpType as ALU, ActivationFunctionType as ACT
 C, S, R = 416, 64, 2
 STEP = [4, 1]
 M = C // 16
-NS = 11
-XD = 4
-NSD = 9
-LO = 2
 H = C // 2
+NS = 18
 BIG = float(2 ** 20)
 B16 = 512.0
+FAR = float(2 ** 90)
 KW = 2048.0
-CWT = 64.0
 DBL = 9
 MA = 14
-HA = 16 * MA
-CUT = 14
-PART = [(16 * CUT, C), (0, 16 * CUT)]
+PART = [(288, C), (144, 288), (0, 144)]
+SHIP = [(144, C), (0, 144)]
+
+TILES = [[0] + list(range(M - 1, M - 4, -1))] + [list(range(m, max(m - 4, 0), -1)) for m in range(M - 4, 0, -4)]
+WIDE = [C] + [max(16 * t[0], 128) for t in TILES[1:]]
+AT = [sum(WIDE[:k]) for k in range(len(TILES))]
+SLOT = {m: (k, j) for k, t in enumerate(TILES) for j, m in enumerate(t)}
 
 F32, BF, F16, U16, I32, X4, U8 = "float32", "bfloat16", "float16", "uint16", "int32", "float8_e4m3fn_x4", "uint8"
 SCRATCH = {}
@@ -27,42 +28,47 @@ def _decl(dtype, cols, names, where="sbuf"):
         SCRATCH[n] = (where, [128, cols], dtype)
 
 
-_decl(BF, 4 * C, "x0 xn z xp z64 dp")
-_decl(BF, 512, "ut vt ones")
-_decl(BF, 2048, "et")
+_decl(BF, 4 * C, "x0 x1 x2 z xs z64 dp")
+_decl(BF, 512, "ut vt grp")
+_decl(BF, 516, "ones et")
+_decl(BF, 1024, "on")
+_decl(BF, 4 * sum(WIDE), "fl")
+_decl(X4, sum(WIDE), "qf0 qf1")
+_decl(U8, sum(WIDE), "sf0 sf1")
 _decl(X4, C, "qx0 qx1 qx2 qz0 qz1 lc0 lc1 rc0 rc1")
 _decl(U8, C, "sx0 sx1 sx2 sz0 sz1 ls0 ls1 rs0 rs1")
 _decl(X4, 128, "uq uq2 vq")
 _decl(U8, 128, "us us2 vs")
+_decl(X4, 256, "oq")
+_decl(U8, 256, "op")
 _decl(X4, 512, "wq eq")
 _decl(U8, 512, "wp es")
 _decl(U16, 32, "li0 li1 ll0 ll1 rl0 rl1")
-_decl(U16, M, "lm lp le cs lq")
+_decl(U16, M, "lm lp lq")
+_decl(U16, C // 4, "le")
 _decl(U16, M * DBL, "lt")
-_decl(U16, 8, "cu lk le2 le3 lcc")
-_decl(F32, C, "p1024 c2 row msk wsc cor ka kb ba bb yy ww elf ybuf")
-_decl(BF, C, "jm dm kp cw ec16 eqf ta tb tp orow posr erow mrow")
-_decl(F16, C, "ex16")
+_decl(U16, 8, "cu lk le2 lcc")
+_decl(U16, S // 4, "le3")
+_decl(F32, C, "p1024 c2 msk wsc ecx ka kb ba bb yy ww elf ybuf")
+_decl(BF, C, "jm rr far0 farq kp ec16 ec4 ta tb tp orow posr erow mrow")
+_decl(F16, C, "ex16 ex4 cor")
 _decl(F16, S, "ex17")
-_decl(BF, C * (M - NSD), "fl")
-_decl(BF, H * (M - NSD), "res")
+_decl(F16, H * (M - 1 - NS), "res")
 _decl(BF, C * 3, "sfl")
 _decl(BF, 128, "pat")
-_decl(F32, 32, "accl accg t1 t2 cb0 cb1 iw cols pal pag pt1 pt2 pcb kc cc")
+_decl(F32, 32, "acc t1 base cols kc cc")
 _decl(I32, 64, "s32")
-_decl(I32, 8, "pc")
+_decl(I32, 16, "pc r4")
 _decl(F32, 72, "endb")
 _decl(F32, S, "zz se seg ex2 ec ec2")
 _decl(F32, 4 * S, "sj")
-_decl(F32, 16 * XD, "prow pmsk pwsc pcor")
-_decl(BF, 16 * XD, "peq")
 _decl(BF, S, "e2r e3r")
 _decl(F32, 512, "psa psb pse psf", "psum")
 _decl(F32, 2048, "psd", "psum")
 
-POOL = {"v": 48, "s": 36, "t": 12, "g": 8}
+POOL = {"v": 48, "s": 32, "t": 12, "g": 10}
 SEMAPHORES = [e + str(k) for e in POOL for k in range(POOL[e])]
-SEMAPHORES += ["d%d" % k for k in range(18)]
+SEMAPHORES += ["d%d" % k for k in range(20)]
 SEMAPHORES += ["sent"] + [n + str(t) for t in range(R) for n in ("ac", "al", "hc", "hs", "hl")]
 
 
@@ -72,7 +78,7 @@ def helpers_of(T, topo, r, t):
         return []
     c = [k for k in topo.cores_of(src) if T.rank_of(k) is None and topo.may_write(k, dst)]
     c.sort(key=lambda k: topo.die(k) != topo.die(src))
-    return c[:len(PART)]
+    return c[:len(SHIP)]
 
 
 def send(g, T, topo, src, dst, out_ap, in_ap, sem):
@@ -90,14 +96,14 @@ def helper_program(g, core, T, topo):
                 continue
             src, dst = T.cores[r], T.cores[r ^ STEP[t]]
             n = len(topo.engines(src, core))
-            a, e = PART[h.index(core)]
+            a, e = SHIP[h.index(core)]
             g.wait_ge(T.sem["hc%d" % t], n)
             total += send(g, T, topo, core, dst, T["lc%d" % t][:, a:e].bitcast(dt.uint8), T["rc%d" % t][:, a:e].bitcast(dt.uint8), "ac%d" % t)
             g.wait_ge(T.sem["hs%d" % t], n)
             total += send(g, T, topo, core, dst, T["ls%d" % t][:, a:e], T["rs%d" % t][:, a:e], "ac%d" % t)
             if core == h[0]:
                 g.wait_ge(T.sem["hl%d" % t], n)
-                total += send(g, T, topo, core, dst, T["ll%d" % t][:, LO:LO + M - XD], T["rl%d" % t][:, LO:LO + M - XD], "al%d" % t)
+                total += send(g, T, topo, core, dst, T["ll%d" % t][:, 0:M], T["rl%d" % t][:, 0:M], "al%d" % t)
     if total:
         g.wait_ge(T.sem["sent"], total)
 
@@ -186,9 +192,9 @@ def rank_program(g, core, T, topo):
         order.append(sem)
         return tok
 
-    def op(e, fn, outs, ins):
+    def op(e, fn, outs, ins, adds=False):
         reads, writes = regs(ins), regs(outs)
-        before(e, reads, writes)
+        before(e, reads, [] if adds else writes)
         sem = e + str(turn[e] % POOL[e])
         turn[e] += 1
         if sem in last:
@@ -237,7 +243,7 @@ def rank_program(g, core, T, topo):
         return op("v", lambda: g.vector.tensor_tensor(o[0], a[0], b[0], f), [o], [a, b])
 
     def scan(o, a, b, init, f0, f1):
-        return op("v", lambda: g.vector.tensor_tensor_scan(o[0], a[0], b[0], init, f0, f1), [o], [a, b])
+        return op("v", lambda: g.vector.tensor_tensor_scan(o[0], a[0], b[0], ap(init), f0, f1), [o], [a, b, init])
 
     def mset(o, v):
         return op("v", lambda: g.vector.memset(o[0], v), [o], [])
@@ -253,28 +259,44 @@ def rank_program(g, core, T, topo):
             kw["accum_out"] = acc[0]
         return op("s", lambda: g.scalar.activation(o[0], i[0], f, **kw), [o, acc], [i, scale, bias])
 
-    def mm(o, w, ws, x, xs):
-        return op("t", lambda: g.tensor.matmul_mx(o[0], w[0], ws[0], x[0], xs[0], True, True), [o], [w, ws, x, xs])
+    def mm(o, w, ws, x, xs, start=True, stop=True):
+        return op("t", lambda: g.tensor.matmul_mx(o[0], w[0], ws[0], x[0], xs[0], start, stop), [o], [w, ws, x, xs], adds=not start)
 
-    QC, QM1, Q63, OFF, OFF16 = [A("cols", k, k + 1) for k in range(5)]
+    def iota(o, pattern, base, step=0):
+        small = {} if SCRATCH[o[1][0][0]][2] == I32 else {"allow_small_or_imprecise_dtypes": True}
+        return op("g", lambda: g.iota(o[0], pattern, base, step, **small), [o], [])
 
-    def scan16(rowv, a=0, e=C, buf="ex16"):
-        scan(A(buf, a, e), rowv, A("ec16", a, e), -B16, ALU.max, ALU.add)
+    def col(k):
+        return A("cols", k, k + 1)
+
+    QC, QM1, Q4, Q4M1, B4, PG, OFF, OFF16, OFF4 = [col(k) for k in (0, 1, 2, 6, 7, 8, 9, 10, 11)]
+
+    def scan16(rowv, a=0, e=C, buf="ex16", ec="ec16"):
+        scan(A(buf, a, e), rowv, A(ec, a, e), -B16, ALU.max, ALU.add)
 
     def list16(lst, a=0, e=C, buf="ex16"):
         ts(lst, A(buf, a + 15, e, 16), OFF16, ALU.subtract)
 
+    def list4(lst, a, e, buf):
+        ts(lst, A(buf, a + 3, e, 4), 4.0, ALU.mult, OFF4, ALU.subtract)
+
     def ship(t, h):
         mine = helpers_of(T, topo, rank, t)
         if mine:
-            a, e = PART[h]
+            a, e = SHIP[h]
             rsend(mine[h], b8(A("rc%d" % t, a, e)), b8(A("qx%d" % t, a, e)), "hc%d" % t)
             rsend(mine[h], A("rs%d" % t, a, e), A("sx%d" % t, a, e), "hs%d" % t)
-        elif h == len(PART) - 1:
+        elif h == len(SHIP) - 1:
             rsend(T.cores[rank ^ STEP[t]], b8(A("lc%d" % t)), b8(A("qx%d" % t)), "ac%d" % t)
             rsend(T.cores[rank ^ STEP[t]], A("ls%d" % t), A("sx%d" % t), "ac%d" % t)
 
-    nss = [NSD if helpers_of(T, topo, rank, t) else NS for t in range(R)]
+    def flags(m, a=0, e=None):
+        k, j = SLOT[m]
+        e = (16 * m if m else C) if e is None else e
+        return A("fl", 4 * (AT[k] + a) + j, 4 * (AT[k] + e), 4)
+
+    def pad(k):
+        return A("fl", 4 * (AT[k] + (16 * TILES[k][-1] if len(TILES[k]) == 4 else 0)), 4 * (AT[k] + WIDE[k]))
 
     dma("y", A("ut"), T.u[:])
     tx1 = dma("s", A("x0", 2 * C, 4 * C), T.x[:, 2 * C:4 * C])
@@ -285,46 +307,49 @@ def rank_program(g, core, T, topo):
     dma("y", b8(A("wq")), T.wc[:])
     dma("y", A("wp"), T.ws[:])
 
-    op("g", lambda: g.iota(T.pc[:, 0:2], [[-1, 2]], 16, 1), [A("pc", 0, 2)], [])
-    op("g", lambda: g.iota(T.s32[:], [[1, 64]], 0, 0), [A("s32")], [])
-    op("g", lambda: g.iota(T.jm[:], [[1, C]], -H, 0, allow_small_or_imprecise_dtypes=True), [A("jm")], [])
-    mset(A("accl", 0, 1), 0.0)
-    mset(A("endb", 0, 1), -1.0)
-    ts(A("pc", 2, 4), A("pc", 0, 2), 15, ALU.bitwise_and)
-    cp(A("cols", 0, 2), A("pc", 2, 4))
-    r16 = A("s32", 0, 16)
-    ts(A("pat", 16, 32), r16, 0.0, ALU.not_equal)
-    ts(A("pat", 0, 16), r16, QC, ALU.is_equal)
-    ts(A("lq"), A("s32", 0, M), 0.0, ALU.mult, QC, ALU.add)
-    ts(Q63, QC, 0.0, ALU.is_gt, CWT - 1.0, ALU.mult)
-    ts(A("cols", 5, 6), QC, 0.0, ALU.is_gt, 2.0, ALU.mult)
-    act(A("dm"), ind(A("pat", 0, 16), A("lq")), ACT.Copy)
-    act(A("kp"), ind(A("pat", 16, 32), A("lq")), ACT.Copy)
-    ts(A("pat", 80, 96), r16, QC, ALU.is_equal, Q63, ALU.mult)
-    ts(A("pat", 96, 112), r16, QM1, ALU.is_equal, -2.0, ALU.mult)
-    ts(A("cu"), A("s32", 0, 8), 16.0, ALU.mult)
-    tt(A("pat", 32, 48), A("pat", 80, 96), A("pat", 16, 32), ALU.add)
-    tt(A("pat", 48, 64), A("pat", 96, 112), A("pat", 0, 16), ALU.add)
-    act(A("cw"), ind(A("pat", 32, 48), A("lq")), ACT.Copy)
-    act(A("ec16"), ind(A("pat", 48, 64), A("lq")), ACT.Copy, scale=B16)
-    ts(A("cs"), A("s32", 0, M), 16.0, ALU.mult, 15.0, ALU.add)
-    for t in range(R):
-        ts(A("cb%d" % t, 0, nss[t]), A("s32", 0, nss[t]), 16.0, ALU.mult)
-        mset(A("cb%d" % t, nss[t], M), float(H))
-    ts(A("pcb", 0, XD), A("s32", M - XD, M), 16.0, ALU.mult)
-    ts(OFF, A("cols", 5, 6), 1.0, ALU.subtract, BIG, ALU.mult)
-    ts(OFF16, A("cols", 5, 6), B16, ALU.mult, B16 + H, ALU.subtract)
-    ts(A("kc", 4, 8), A("s32", 0, 4), 16.0, ALU.mult, QC, ALU.add)
+    iota(A("pc", 0, 5), [[-1, 5]], 16, 1)
+    iota(A("s32"), [[1, 64]], 0)
+    iota(A("rr"), [[0, M], [1, 16]], 0)
+    iota(A("grp"), [[1, 8], [0, 64]], 1)
+    iota(A("jm"), [[1, C]], -H)
     mset(A("ones"), 1.0)
-    ts(A("kc", 0, 4), A("kc", 4, 8), 0.5, ALU.subtract)
-    tt(A("zz"), A("s32"), A("dm", 0, S), ALU.mult)
+    ts(A("pc", 5, 7), A("pc", 0, 2), 15, ALU.bitwise_and)
+    ts(A("pc", 7, 12), A("pc", 0, 5), 2, ALU.logical_shift_right, 3, ALU.bitwise_and)
+    ts(A("pc", 12, 13), A("pc", 0, 1), 3, ALU.bitwise_and)
+    ts(A("pc", 13, 14), A("pc", 0, 1), 4, ALU.logical_shift_right)
+    ts(A("cu"), A("s32", 0, 8), 16.0, ALU.mult)
+    mset(pad(0), 0.0)
+    cp(A("cols", 0, 9), A("pc", 5, 14))
+    for k in range(1, 5):
+        mset(pad(k), 0.0)
+    for k in range(5, len(TILES)):
+        n = 4 * WIDE[k] - (64 * TILES[k][-1] if len(TILES[k]) == 4 else 0)
+        act(pad(k), A("ones", 0, n), ACT.Copy, scale=0.0)
+    r16 = A("s32", 0, 16)
+    ts(A("pat", 0, 16), r16, QC, ALU.is_equal)
+    ts(A("pat", 16, 32), r16, QM1, ALU.is_equal, -2.0, ALU.mult)
+    ts(A("lq"), A("s32", 0, M), 0.0, ALU.mult, QC, ALU.add)
+    ts(A("farq"), A("rr"), QC, ALU.not_equal, FAR, ALU.mult)
+    tt(A("pat", 32, 48), A("pat", 0, 16), A("pat", 16, 32), ALU.add)
+    ts(A("far0"), A("rr"), 0.0, ALU.is_equal, FAR, ALU.mult)
+    act(A("ec16"), ind(A("pat", 32, 48), A("lq")), ACT.Copy, scale=B16)
+    act(col(12), QC, ACT.Sign)
+    act(col(13), A("pat", 47, 48), ACT.Identity, scale=B16, bias=QC)
+    act(OFF16, col(12), ACT.Identity, scale=2 * B16, bias=-B16 - H)
     quant(A("uq"), A("us"), A("ut"))
+    ts(A("kp"), A("rr"), 0.0, ALU.not_equal)
     op("v", lambda: g.vector.tensor_copy(T.uq2[:, 0:128].bitcast(dt.uint32), T.uq[:, 0:128].bitcast(dt.uint32).indirect(T.cu[:, 0:8])),
        [A("uq2")], [A("uq"), A("cu")])
     op("s", lambda: g.scalar.activation(T.us2[:, 0:128], T.us[:, 0:128].indirect(T.cu[:, 0:8]), ACT.Copy), [A("us2")], [A("us"), A("cu")])
     quant(A("qx0", H, C), A("sx0", H, C), A("x0", 2 * C, 4 * C))
     quant(A("qx0", 0, H), A("sx0", 0, H), A("x0", 0, 2 * C))
-    for h in range(len(PART)):
+    ts(A("on", 0, 512), A("grp"), PG, ALU.is_equal)
+    ts(A("on", 512, 1024), A("grp"), PG, ALU.is_equal)
+    act(A("ecx"), A("ec16"), ACT.Copy)
+    act(A("on", 512, 1024, 4), A("on", 0, 512, 4), ACT.Copy, scale=-1.0)
+    mset(A("acc", 0, 1), 0.0)
+    mset(A("endb", 0, 1), -1.0)
+    for h in range(len(SHIP)):
         ship(0, h)
 
     for t in range(R):
@@ -333,124 +358,151 @@ def rank_program(g, core, T, topo):
         theirs = helpers_of(T, topo, rank ^ STEP[t], t)
         qx, sx = "qx%d" % t, "sx%d" % t
         li, ll, lc, ls = "li%d" % t, "ll%d" % t, "lc%d" % t, "ls%d" % t
-        qz, sz = "qz%d" % t, "sz%d" % t
-        ns, cb = nss[t], "cb%d" % t
-        me = M - XD if mine else M
+        qz, sz, qf, sf = "qz%d" % t, "sz%d" % t, "qf%d" % t, "sf%d" % t
 
         mm(A("psa", 0, C), A("uq2"), A("us2"), A(qx), A(sx))
         mm(A("psb", 0, C), A("uq2"), A("us2"), A(qx), A(sx))
         srcs = theirs if theirs else [partner]
         arrive("ac%d" % t, sum(2 * len(topo.engines(k, core)) for k in srcs), [A(lc), A(ls)])
-        arrive("al%d" % t, len(topo.engines(srcs[0], core)), [A(ll, LO, LO + me)])
+        arrive("al%d" % t, len(topo.engines(srcs[0], core)), [A(ll, 0, M)])
         if t == 0:
-            for b in range(4):
-                op("g", lambda: g.affine_select(T.et[:, 512 * b:512 * b + 512], T.ones[:], [[-1, 512]], ALU.is_equal, 0.0, b, 4),
-                   [A("et", 512 * b, 512 * b + 512)], [A("ones")])
+            op("g", lambda: g.affine_select(T.et[:], T.ones[:], [[-1, 516]], ALU.is_equal, 0.0, 3, 4), [A("et")], [A("ones")])
 
-        cut = 16 * ns
-        tt(A("msk", 0, cut), A("psa", 0, cut), A("dm", 0, cut), ALU.mult)
-        act(A("row"), A("psb", 0, C), ACT.Copy)
-        tt(A("msk", cut, C), A("psa", cut, C), A("dm", cut, C), ALU.mult)
-        scan(A("wsc", 0, cut), A("kp", 0, cut), A("msk", 0, cut), 0.0, ALU.mult, ALU.add)
-        scan(A("wsc", cut, C), A("kp", cut, C), A("msk", cut, C), 0.0, ALU.mult, ALU.add)
+        def own_mask(a, e):
+            tt(A("msk", a, e), A("psa", a, e), A("farq", a, e), ALU.add)
 
-        def s_blocks(blocks, bank, w, accl, accg):
-            def first(k):
-                o = (k % 3) * C
-                act(A("sfl", o, o + C), A(bank, 0, C), ACT.Sign, scale=-1.0, bias=A(w, 16 * k + 15, 16 * k + 16))
+        def own_scan(a, e):
+            scan(A("wsc", a, e), A("far0", a, e), A("msk", a, e), 0.0, ALU.add, ALU.min)
 
-            first(0)
-            for k, m in enumerate(blocks):
-                if k + 1 < len(blocks):
-                    first(k + 1)
-                o = (k % 3) * C
-                if m:
-                    act(A("sfl", o, o + 16 * m), A("sfl", o, o + 16 * m), ACT.Relu, acc=A(accl, k, k + 1))
-                act(A("sfl", o + 16 * m, o + C), A("sfl", o + 16 * m, o + C), ACT.Relu, scale=-1.0, acc=A(accg, k, k + 1))
+        def own(m):
+            return A("wsc", 16 * m + 15, 16 * m + 16)
+
+        def s_first(m):
+            o = (m % 3) * C
+            act(A("sfl", o, o + 16 * m), A("psb", 0, 16 * m), ACT.Sign, scale=-1.0, bias=own(m))
+
+        def s_second(m):
+            o = (m % 3) * C
+            act(flags(m), A("sfl", o, o + 16 * m), ACT.Relu, acc=A("acc", m, m + 1))
+
+        def s_tile(k):
+            for m in TILES[k]:
+                if m > 1:
+                    s_first(m - 1)
+                s_second(m)
 
         def v_first(m):
-            o, w = (m - ns) * C, A("wsc", 16 * m + 15, 16 * m + 16)
-            ts(A("fl", o, o + 16 * m), A("psa", 0, 16 * m), w, ALU.is_ge)
-            ts(A("fl", o + 16 * m, o + C), A("psa", 16 * m, C), w, ALU.is_gt)
+            ts(flags(m), A("psa", 0, 16 * m), own(m), ALU.is_lt)
 
         def v_second(m):
-            o, k = (m - ns) * C, (m - ns) * H
-            scan(A("res", k, k + H), A("fl", o, o + H), A("fl", o + H, o + C), -float(H), ALU.add, ALU.add)
+            e = H * (m - NS)
+            scan(A("res", e - 8 * m, e), flags(m, 0, 8 * m), flags(m, 8 * m), 0.0, ALU.add, ALU.add)
 
-        def v_sum(m0, m1):
-            tt(A("iw", m0, m1), A("t2", m0, m1), A("res", H * (m0 - ns) + H - 1, H * (m1 - ns), H), ALU.add)
+        def pack(k):
+            a, e = AT[k], AT[k] + WIDE[k]
+            quant(A(qf, a, e), A(sf, a, e), A("fl", 4 * a, 4 * e))
 
-        s_blocks(list(range(ns)), "psb", "wsc", "accl", "accg")
-        tt(A("eqf"), ind(A("wsc"), A("cs")), A("row"), ALU.is_equal)
-        v_first(ns)
-        scan(A("cor"), A("cw"), A("eqf"), 0.0, ALU.mult, ALU.add)
-        for m in range(ns, me):
-            if m + 1 < me:
-                v_first(m + 1)
-            if m == ns:
-                ts(A("t1", 0, M), A("cor", 15, C, 16), 1.0 / CWT, ALU.mult)
-            if m == ns + 1:
-                tt(A("t2", 0, M), A("t1", 0, M), A(cb, 0, M), ALU.add)
-            v_second(m)
-        tt(A("t1", 0, ns), A("t2", 0, ns), A("accl", 0, ns), ALU.subtract)
-        v_sum(ns, me)
-        tt(A("iw", 0, ns), A("t1", 0, ns), A("accg", 0, ns), ALU.add)
-        cp(A(li, LO, LO + me), A("iw", 0, me))
-        if mine:
-            rsend(mine[0], A("rl%d" % t, LO, LO + me), A(li, LO, LO + me), "hl%d" % t)
-        else:
-            rsend(partner, A(ll, LO, LO + me), A(li, LO, LO + me), "al%d" % t)
+        def total(k, start=False, stop=False):
+            a, e, o = AT[k], AT[k] + WIDE[k], 0 if k else 128
+            mm(A("pse", 0, e - a), A("oq", o, o + 128), A("op", o, o + 128), A(qf, a, e), A(sf, a, e), start, stop)
 
-        if mine:
-            n = 16 * XD
-            mm(A("psf", 0, 128), A("uq2"), A("us2"), A(lc, C - 128, C), A(ls, C - 128, C))
-            mm(A("pse", 0, C), A("uq2"), A("us2"), A(lc), A(ls))
-            tt(A("pmsk"), A("psf", 128 - n, 128), A("dm", 0, n), ALU.mult)
-            act(A("prow"), A("pse", C - n, C), ACT.Copy)
-            scan(A("pwsc"), A("kp", 0, n), A("pmsk"), 0.0, ALU.mult, ALU.add)
-            v_first(me)
-            s_blocks(list(range(me, M)), "pse", "pwsc", "pal", "pag")
-            for m in range(me, M):
-                if m + 1 < M:
-                    v_first(m + 1)
-                if m == me:
-                    tt(A("peq"), ind(A("pwsc"), A("cs", 0, XD)), A("prow"), ALU.is_equal)
-                if m == me + 1:
-                    scan(A("pcor"), A("cw", 0, n), A("peq"), 0.0, ALU.mult, ALU.add)
-                if m == me + 2:
-                    ts(A("pt1", 0, XD), A("pcor", 15, n, 16), 1.0 / CWT, ALU.mult)
-                if m == me + 3:
-                    tt(A("pt2", 0, XD), A("pt1", 0, XD), A("pcb", 0, XD), ALU.add)
-                v_second(m)
-            v_sum(me, M)
-            cp(A(li, LO + me, LO + M), A("iw", me, M))
-        scatter(A("orow"), A(li, LO, LO + M), A("jm"))
-        if mine:
-            tt(A("pt1", 0, XD), A("pt2", 0, XD), A("pal", 0, XD), ALU.subtract)
-            tt(A("pt2", 0, XD), A("pt1", 0, XD), A("pag", 0, XD), ALU.add)
-            cp(A(ll, LO + me, LO + M), A("pt2", 0, XD))
+        c1, c2 = 16 * (NS - 4), 16 * (NS + 1)
+        own_mask(c1, c2)
+        own_mask(c2, C)
+        own_scan(c1, c2)
+        own_mask(0, c1)
+        own_scan(c2, C)
+        s_first(NS)
+        s_tile(2)
+        own_scan(0, c1)
+        v_first(M - 1)
+        v_first(M - 2)
+        tt(flags(0), A("psa", 0, C), A("wsc"), ALU.is_gt)
+        v_first(M - 3)
         if t == 0:
-            act(A("p1024"), A("jm"), ACT.Identity, scale=KW, bias=KW * H)
-            act(A("c2"), A("jm"), ACT.Identity, scale=KW, bias=KW * (H - 1))
+            quant(A("oq"), A("op"), A("on"))
+            ts(A("base", 0, M), A("jm", 0, C, 16), col(13), ALU.add)
+        v_second(M - 1)
+        pack(0)
+        total(0, start=True)
+        s_tile(3)
+        v_first(M - 4)
+        pack(2)
+        total(2)
+        v_first(M - 5)
+        scan(A("cor"), A("kp"), flags(0), 0.0, ALU.mult, ALU.add)
+        v_first(M - 6)
+        s_tile(4)
+        pack(3)
+        total(3)
+        v_first(M - 7)
+        tt(A("t1", 0, M), A("base", 0, M), A("cor", 15, C, 16), ALU.add)
+        v_second(M - 2)
+        pack(1)
+        total(1)
+        s_tile(5)
+        pack(4)
+        total(4)
+        s_tile(6)
+        v_second(M - 3)
+        v_second(M - 4)
+        pack(5)
+        total(5)
+        v_second(M - 5)
+        pack(6)
+        total(6, stop=True)
+        v_second(M - 6)
+        v_second(M - 7)
+        tt(A("ecx", 15, c2, 16), A("t1", 0, NS + 1), A("acc", 0, NS + 1), ALU.subtract)
+        tt(A("ecx", c2 + 15, C, 16), A("t1", NS + 1, M), A("res", H - 1, H * (M - 1 - NS), H), ALU.subtract)
+        scan16(A("pse", 0, C), ec="ecx")
+        list16(A(li, 0, M))
+        if mine:
+            rsend(mine[0], A("rl%d" % t, 0, M), A(li, 0, M), "hl%d" % t)
+        else:
+            rsend(partner, A(ll, 0, M), A(li, 0, M), "al%d" % t)
+
+        scatter(A("orow"), A(li, 0, M), A("jm"))
+        if t == 0:
+            iota(A("p1024"), [[int(KW), C]], 0)
+            iota(A("c2"), [[int(KW), C]], -int(KW))
+            for b in range(4):
+                quant(A("eq", 128 * b, 128 * b + 128), A("es", 128 * b, 128 * b + 128), A("et", 3 - b, 515 - b))
+            ts(A("r4"), r16, 3, ALU.bitwise_and)
+            ts(A("kc", 4, 8), A("s32", 0, 4), 16.0, ALU.mult, QC, ALU.add)
+            ts(A("pat", 48, 64), A("r4"), Q4, ALU.is_equal)
+            ts(A("pat", 64, 80), A("r4"), Q4M1, ALU.is_equal, -2.0, ALU.mult)
             act(A("ec"), A("ec16", 0, S), ACT.Copy, scale=BIG / B16)
-            for b in range(2):
-                act(A("xp", b * C, b * C + C), A("x0", b, 4 * C, 4), ACT.Copy, scale=64.0)
-            quant(A("eq"), A("es"), A("et"))
+            act(A("kc", 0, 4), A("kc", 4, 8), ACT.Identity, bias=-0.5)
+            act(OFF, col(12), ACT.Identity, scale=2 * BIG, bias=-BIG)
+            act(col(14), Q4, ACT.Sign)
+            act(col(15), B4, ACT.Identity, scale=-1.0, bias=-4 * (B16 + H))
+            act(OFF4, col(14), ACT.Identity, scale=8 * B16, bias=col(15))
+        else:
+            quant(A("vq"), A("vs"), A("vt"))
         for b in range(4):
             mm(A("psd", 512 * b, 512 * b + C), A("eq", 128 * b, 128 * b + 128), A("es", 128 * b, 128 * b + 128), A(lc), A(ls))
 
+        def unpack(b):
+            act(A("dp", b, 4 * C, 4), A("psd", 512 * b, 512 * b + C), ACT.Copy)
+
+        if t:
+            for b in range(4):
+                unpack(b)
+
         tb_, kb_, bb_ = ["ta", "tb"], ["ka", "kb"], ["ba", "bb"]
-        act(A("tp"), ind(A("orow"), A(ll, LO, LO + M)), ACT.Copy)
-        ts(A("ka"), ind(A("orow"), A(ll, LO, LO + M)), KW, ALU.mult, KW * H + 1.0, ALU.add)
-        act(A("ba"), A("tp"), ACT.Identity, scale=KW, bias=KW * H + 2.0)
-        scan16(A("tp"))
-        list16(A("lt", 0, M))
         halves = [(0, MA), (MA, M)]
-        for k in range(DBL):
+        for c, e in halves:
+            act(A("tp", 16 * c, 16 * e), ind(A("orow"), A(ll, c, e)), ACT.Copy)
+        for c, e in halves:
+            ts(A("ka", 16 * c, 16 * e), ind(A("orow"), A(ll, c, e)), KW, ALU.mult, KW * H + 1.0, ALU.add)
+        for c, e in halves:
+            scan16(A("tp", 16 * c, 16 * e), 16 * c, 16 * e)
+        for c, e in halves:
+            list16(A("lt", c, e), 16 * c, 16 * e)
+        act(A("ba"), A("tp"), ACT.Identity, scale=KW, bias=KW * H + 2.0)
+        for k in range(DBL - 1):
             a, b = k % 2, (k + 1) % 2
-            if k + 1 == DBL:
-                tt(A(kb_[b]), ind(A(bb_[a]), A("lt", k * M, k * M + M)), A(kb_[a]), ALU.min)
-                break
             for c, e in halves:
                 act(A(tb_[b], 16 * c, 16 * e), ind(A(tb_[a] if k else "tp"), A("lt", k * M + c, k * M + e)), ACT.Copy)
             for c, e in halves:
@@ -461,137 +513,156 @@ def rank_program(g, core, T, topo):
                 list16(A("lt", (k + 1) * M + c, (k + 1) * M + e), 16 * c, 16 * e)
             for c, e in halves:
                 act(A(bb_[b], 16 * c, 16 * e), A(kb_[b], 16 * c, 16 * e), ACT.Identity, bias=float(2 ** (k + 1)))
-        K = A(kb_[DBL % 2])
 
-        def unpack(b):
-            act(A("dp", b * C, b * C + C), A("psd", 512 * b, 512 * b + C), ACT.Copy)
-
-        unpack(0)
-        act(A("mrow"), K, ACT.Identity, scale=1.0 / KW, bias=-float(H))
-        unpack(1)
-        unpack(2)
-        scan(A("yy"), K, A("p1024"), 0.0, ALU.max, ALU.max)
-        if t == 0:
-            tt(A("ec2"), A("ec"), A("zz"), ALU.subtract)
-        else:
-            quant(A("vq"), A("vs"), A("vt"))
-        scan(A("ww"), A("yy"), A("c2"), -KW - H, ALU.add, ALU.subtract)
-        scan16(A("mrow"))
+        k = DBL - 1
+        kn = kb_[DBL % 2]
+        HA = 16 * MA
+        for c, e in halves:
+            tt(A(kn, 16 * c, 16 * e), ind(A(bb_[k % 2]), A("lt", k * M + c, k * M + e)), A(kb_[k % 2], 16 * c, 16 * e), ALU.min)
+            act(A("mrow", 16 * c, 16 * e), A(kn, 16 * c, 16 * e), ACT.Identity, scale=1.0 / KW, bias=-float(H))
+        for c, e in halves:
+            scan(A("yy", 16 * c, 16 * e), A(kn, 16 * c, 16 * e), A("p1024", 16 * c, 16 * e), 0.0, ALU.max, ALU.max)
+        scan(A("ww", 0, HA), A("yy", 0, HA), A("c2", 0, HA), -KW - H, ALU.add, ALU.subtract)
+        scan16(A("mrow", 0, HA), 0, HA)
         scan(A("endb", 1, S + 1), A("yy", 0, S), A("p1024", 0, S), -1.0, ALU.add, ALU.subtract)
-        list16(A("lm"))
+        scan(A("ww", HA, C), A("yy", HA, C), A("c2", HA, C), A("ww", HA - 1, HA), ALU.add, ALU.subtract)
+        list16(A("lm", 0, MA), 0, HA)
+        scan16(A("mrow", HA, C), HA, C)
         for m in range(4):
             act(A("sj", S * m, S * m + S), A("endb", 1, S + 1), ACT.Sign, scale=-1.0, bias=A("kc", m, m + 1), acc=A("cc", m, m + 1))
-        unpack(3)
         tt(A("se"), A("endb", 0, S), A("endb", 1, S + 1), ALU.add)
-        tt(A("posr"), ind(A("ww"), A("lm")), K, ALU.subtract)
+        if t == 0:
+            tt(A("pat", 80, 96), A("pat", 48, 64), A("pat", 64, 80), ALU.add)
+            ts(A("zz"), A("rr", 0, S), QC, ALU.is_equal)
+        tt(A("posr", 0, HA), ind(A("ww"), A("lm", 0, MA)), A(kn, 0, HA), ALU.subtract)
+        list16(A("lm", MA, M), HA, C)
+        if t == 0:
+            act(A("ec4"), ind(A("pat", 80, 96), A("lq")), ACT.Copy, scale=B16)
+            tt(A("zz"), A("zz"), A("s32"), ALU.mult)
         ts(A("lcc", 0, 4), A("cc", 0, 4), float(S), ALU.add, 0.5, ALU.mult)
-        scan16(A("posr"))
+        scan16(A("posr", 0, HA), 0, HA)
+        tt(A("posr", HA, C), ind(A("ww"), A("lm", MA, M)), A(kn, HA, C), ALU.subtract)
         act(A("seg"), ind(A("se"), A("lcc", 0, 4)), ACT.Identity, bias=1.0)
         if t == 0:
-            for b in range(2, 4):
-                act(A("xp", b * C, b * C + C), A("x0", b, 4 * C, 4), ACT.Copy, scale=64.0)
-        list16(A("lp"))
+            tt(A("ec2"), A("ec"), A("zz"), ALU.subtract)
+            for b in range(4):
+                unpack(b)
+        list16(A("lp", 0, MA), 0, HA)
+        scan16(A("posr", HA, C), HA, C)
         scan(A("ex2"), A("seg"), A("ec2"), -BIG, ALU.max, ALU.add)
-        scatter(A("erow"), A("lp"), A("jm"))
+        list16(A("lp", MA, M), HA, C)
         ts(A("lk", 0, 4), A("ex2", 15, S, 16), OFF, ALU.subtract)
-        scan16(A("erow"))
-        cp(A("e2r"), ind(A("erow"), A("lk", 0, 4)))
-        list16(A("le"))
-        scan16(A("e2r"), 0, S, "ex17")
+        scatter(A("erow"), A("lp"), A("jm"))
 
-        banks = [[A("psd", 512 * b, 512 * b + PART[0][1] - PART[0][0]) for b in range(4)],
-                 [A(n, 0, PART[1][1]) for n in ("psa", "psb", "pse", "psf")]]
-        nx, ns_ = "qx%d" % (t + 1), "sx%d" % (t + 1)
+        banks = [[A("psd", 512 * b, 512 * b + PART[h][1] - PART[h][0]) for b in range(4)] for h in (0, 2)]
+        ybank = ("psa", "psb", "pse", "psf")
+        banks.insert(1, [A(n, 0, PART[1][1] - PART[1][0]) for n in ybank])
+        xo, xn, nx, ns_ = "x%d" % t, "x%d" % (t + 1), "qx%d" % (t + 1), "sx%d" % (t + 1)
+
+        def run(name, h):
+            return A(name, 4 * PART[h][0], 4 * PART[h][1])
 
         def tile(name, h, b):
             return A(name, 4 * PART[h][0] + b, 4 * PART[h][1], 4)
 
-        def plane(name, h, b):
-            return A(name, b * C + PART[h][0], b * C + PART[h][1])
+        def words(a, e):
+            scan16(A("erow", a, e), a, e, "ex4", "ec4")
+
+        def offsets(a, e):
+            list4(A("le", a // 4, e // 4), a, e, "ex4")
+
+        def own_v(a, e):
+            cp(A("z", 4 * a, 4 * e), ind(A(xo), A("le", a // 4, e // 4)))
+
+        def own_s(a, e):
+            act(A("z", 4 * a, 4 * e), ind(A(xo), A("le", a // 4, e // 4)), ACT.Copy)
 
         def layer(h):
             a, e = PART[h]
-            quant(A(qz, a, e), A(sz, a, e), A("z", 4 * a, 4 * e))
+            quant(A(qz, a, e), A(sz, a, e), run("z", h))
             for b in range(4):
                 mm(banks[h][b], A("wq", 128 * b, 128 * b + 128), A("wp", 128 * b, 128 * b + 128), A(qz, a, e), A(sz, a, e))
 
         def finish(h):
             a, e = PART[h]
-            quant(A(nx, a, e), A(ns_, a, e), A("xn", 4 * a, 4 * e))
+            quant(A(nx, a, e), A(ns_, a, e), run(xn, h))
             if t == R - 1:
-                mm(A("psd", 512 * h, 512 * h + e - a), A("vq"), A("vs"), A(nx, a, e), A(ns_, a, e))
+                mm(A(ybank[h], 0, e - a), A("vq"), A("vs"), A(nx, a, e), A(ns_, a, e))
                 dma("y", T.oc[:, 4 * a:4 * e], b8(A(nx, a, e)))
-            else:
-                ship(t + 1, h)
+            elif h:
+                ship(t + 1, h - 1)
 
-        def up_v(h, b):
-            ts(plane("z64", h, b), tile("z", h, b), 64.0, ALU.mult)
+        def store(h):
+            if t == R - 1:
+                a, e = PART[h]
+                act(A("ybuf", a, e), A(ybank[h], 0, e - a), ACT.Copy)
+                dma("s", T.y[:, a:e], A("ybuf", a, e))
 
-        def down_v(h, b):
-            ts(tile("xn", h, b), plane("xp", h, b), 1.0 / 64.0, ALU.mult)
+        def up_v(h):
+            ts(run("z64", h), run("z", h), 64.0, ALU.mult)
 
-        def down_s(h, b):
-            act(tile("xn", h, b), plane("xp", h, b), ACT.Copy, scale=1.0 / 64.0)
+        def up_s(h):
+            act(run("z64", h), run("z", h), ACT.Copy, scale=64.0)
 
-        def add(h, b):
-            tt(plane("xp", h, b), banks[h][b], plane("z64", h, b), ALU.add)
+        def down_v(h, bs=None):
+            for o, i in ([(run(xn, h), run("xs", h))] if bs is None else [(tile(xn, h, b), tile("xs", h, b)) for b in bs]):
+                ts(o, i, 1.0 / 64.0, ALU.mult)
 
-        def own_v(b, c0, c1):
-            ts(A("z", 64 * c0 + b, 64 * c1, 4), ind(A("xp", b * C, b * C + C), A("le", c0, c1)), 1.0 / 64.0, ALU.mult)
+        def down_s(h, bs):
+            for b in bs:
+                act(tile(xn, h, b), tile("xs", h, b), ACT.Copy, scale=1.0 / 64.0)
 
-        def own_s(b, c0, c1):
-            act(A("z", 64 * c0 + b, 64 * c1, 4), ind(A("xp", b * C, b * C + C), A("le", c0, c1)), ACT.Copy, scale=1.0 / 64.0)
+        def add(h, bs=range(4)):
+            for b in bs:
+                tt(tile("xs", h, b), banks[h][b], tile("z64", h, b), ALU.add)
 
-        for b in range(3):
-            own_s(b, CUT, M)
-        for b in range(4):
-            own_s(b, 4, CUT)
-        list16(A("le2", 0, 4), 0, S, "ex17")
-        own_v(3, CUT, M)
-        cp(A("e3r"), ind(A("tp"), A("le2", 0, 4)))
-        up_v(0, 3)
-        scan16(A("e3r"), 0, S, "ex17")
-        up_v(0, 0)
-        list16(A("le3", 0, 4), 0, S, "ex17")
+        a0, a1 = PART[0][0], PART[1][0]
+        mid = (a0 + C) // 2
+        words(a0, C)
+        act(A("e2r"), ind(A("erow"), A("lk", 0, 4)), ACT.Copy)
+        words(S, a0)
+        offsets(a0, C)
+        offsets(S, a0)
+        own_s(mid, C)
+        own_v(a0, mid)
+        scan16(A("e2r"), 0, S, "ex17")
+        own_s(a1, a1 + 72)
         layer(0)
-        for b in range(4):
-            cp(A("z", b, 4 * S, 4), ind(A("dp", b * C, b * C + C), A("le3", 0, 4)))
-        up_v(0, 1)
-        up_v(0, 2)
-        add(0, 0)
-        add(0, 1)
+        list16(A("le2", 0, 4), 0, S, "ex17")
+        up_v(0)
+        act(A("e3r"), ind(A("tp"), A("le2", 0, 4)), ACT.Copy)
+        own_s(a1 + 72, a0)
+        add(0, (0, 1))
+        scan16(A("e3r"), 0, S, "ex17", "ec4")
+        add(0, (2, 3))
+        list4(A("le3"), 0, S, "ex17")
         layer(1)
-        for b in range(4):
-            act(plane("z64", 1, b), tile("z", 1, b), ACT.Copy, scale=64.0)
-        add(0, 2)
-        add(0, 3)
-        down_s(0, 0)
-        down_s(0, 1)
-        down_v(0, 2)
-        down_v(0, 3)
-        add(1, 0)
-        down_s(1, 0)
+        own_s(S, a1)
+        act(A("z", 0, 4 * S), ind(A("dp"), A("le3")), ACT.Copy)
+        up_v(1)
+        down_v(0)
+        add(1, (0, 1))
         finish(0)
-        add(1, 1)
-        down_s(1, 1)
-        add(1, 2)
-        down_s(1, 2)
-        add(1, 3)
-        down_v(1, 3)
-        if t == R - 1:
-            a, e = PART[0]
-            act(A("ybuf", a, e), A("psd", 0, e - a), ACT.Copy)
-            dma("s", T.y[:, a:e], A("ybuf", a, e))
+        layer(2)
+        add(1, (2, 3))
+        up_v(2)
+        down_s(1, range(4))
+        add(2, (0, 1))
         finish(1)
+        store(0)
+        add(2, (2, 3))
+        down_s(2, (0, 1))
+        down_v(2, (2, 3))
+        if t == R - 1:
+            act(A("elf"), A("erow"), ACT.Identity, bias=float(H))
+            dma("y", T.el[:], (T.elf[0:128:16, :], A("elf")[1]))
+        store(1)
+        finish(2)
+        store(2)
 
-    a, e = PART[1]
-    cp(A("ybuf", a, e), A("psd", 512, 512 + e))
-    act(A("elf"), A("erow"), ACT.Identity, bias=float(H))
-    dma("y", T.y[:, a:e], A("ybuf", a, e))
-    dma("s", T.el[:], (T.elf[0:128:16, :], A("elf")[1]))
     sx = "sx%d" % R
     for k in range(4):
-        dma("s", T.osc[4 * k:4 * k + 4, :], (T[sx][32 * k:32 * k + 4, :], A(sx)[1]))
+        dma("y", T.osc[4 * k:4 * k + 4, :], (T[sx][32 * k:32 * k + 4, :], A(sx)[1]))
 
     g.wait_ge(T.sem["sent"], nsent[0])
     done = set()

@@ -1,22 +1,26 @@
-from concourse.mybir import dt, AluOpType as ALU, ActivationFunctionType as ACT
+from concourse.mybir import dt, AluOpType as ALU, ActivationFunctionType as ACT, AxisListType as AX
 
 C, S, R = 416, 64, 2
 STEP = [4, 1]
 M = C // 16
 H = C // 2
 NS = 18
-BIG = float(2 ** 20)
+NV = 2
+BIG = float(2 ** 21)
 B16 = 512.0
 FAR = float(2 ** 90)
 KW = 2048.0
 DBL = 9
 MA = 14
-PART = [(288, C), (144, 288), (0, 144)]
-SHIP = [(144, C), (0, 144)]
+HA = 16 * MA
+LOW = 16 * NS
+PART = [(LOW // 2, LOW), (0, LOW // 2), (LOW, C)]
+VIA = [1, 0, 1]
 
 TILES = [[0] + list(range(M - 1, M - 4, -1))] + [list(range(m, max(m - 4, 0), -1)) for m in range(M - 4, 0, -4)]
 WIDE = [C] + [max(16 * t[0], 128) for t in TILES[1:]]
-AT = [sum(WIDE[:k]) for k in range(len(TILES))]
+NT = len(TILES)
+AT = [sum(WIDE[:k]) for k in range(NT)]
 SLOT = {m: (k, j) for k, t in enumerate(TILES) for j, m in enumerate(t)}
 
 F32, BF, F16, U16, I32, X4, U8 = "float32", "bfloat16", "float16", "uint16", "int32", "float8_e4m3fn_x4", "uint8"
@@ -29,7 +33,7 @@ def _decl(dtype, cols, names, where="sbuf"):
 
 
 _decl(BF, 4 * C, "x0 x1 x2 z xs z64 dp")
-_decl(BF, 512, "ut vt grp")
+_decl(BF, 512, "ut vt")
 _decl(BF, 516, "ones et")
 _decl(BF, 1024, "on")
 _decl(BF, 4 * sum(WIDE), "fl")
@@ -47,29 +51,31 @@ _decl(U16, 32, "li0 li1 ll0 ll1 rl0 rl1")
 _decl(U16, M, "lm lp lq")
 _decl(U16, C // 4, "le")
 _decl(U16, M * DBL, "lt")
-_decl(U16, 8, "cu lk le2 lcc")
+_decl(U16, 8, "cu lk lcc")
 _decl(U16, S // 4, "le3")
-_decl(F32, C, "p1024 c2 msk wsc ecx ka kb ba bb yy ww elf ybuf")
-_decl(BF, C, "jm rr far0 farq kp ec16 ec4 ta tb tp orow posr erow mrow")
-_decl(F16, C, "ex16 ex4 cor")
+_decl(F32, C, "p1024 msk wsc exk ka kb ba bb yy elf ybuf")
+_decl(BF, C, "jm rr far0 farq kp ec16 ec4 eck ta tb tp orow posr erow")
+_decl(F16, C, "ex16 ex4 ecx cor")
 _decl(F16, S, "ex17")
 _decl(F16, H * (M - 1 - NS), "res")
 _decl(BF, C * 3, "sfl")
-_decl(BF, 128, "pat")
-_decl(F32, 32, "acc t1 base cols kc cc")
+_decl(BF, 128, "pat grp")
+_decl(F32, 32, "acc t1 t2 base cols kc cc")
 _decl(I32, 64, "s32")
 _decl(I32, 16, "pc r4")
-_decl(F32, 72, "endb")
-_decl(F32, S, "zz se seg ex2 ec ec2")
-_decl(F32, 4 * S, "sj")
-_decl(BF, S, "e2r e3r")
+_decl(F32, C + 8, "ww")
+_decl(F32, S, "seg ex2 ec2")
+_decl(F32, 2 * S + 8, "se")
+_decl(F32, 4 * S + 8, "sj")
+_decl(BF, S, "e3r")
 _decl(F32, 512, "psa psb pse psf", "psum")
 _decl(F32, 2048, "psd", "psum")
 
 POOL = {"v": 48, "s": 32, "t": 12, "g": 10}
 SEMAPHORES = [e + str(k) for e in POOL for k in range(POOL[e])]
 SEMAPHORES += ["d%d" % k for k in range(20)]
-SEMAPHORES += ["sent"] + [n + str(t) for t in range(R) for n in ("ac", "al", "hc", "hs", "hl")]
+SEMAPHORES += ["sent"] + [n + str(t) for t in range(R) for n in ("ac", "al", "hl")]
+SEMAPHORES += ["%s%d_%d" % (n, t, h) for t in range(R) for n in ("hc", "hs") for h in range(len(PART))]
 
 
 def helpers_of(T, topo, r, t):
@@ -78,7 +84,7 @@ def helpers_of(T, topo, r, t):
         return []
     c = [k for k in topo.cores_of(src) if T.rank_of(k) is None and topo.may_write(k, dst)]
     c.sort(key=lambda k: topo.die(k) != topo.die(src))
-    return c[:len(SHIP)]
+    return c[:max(VIA) + 1]
 
 
 def send(g, T, topo, src, dst, out_ap, in_ap, sem):
@@ -91,17 +97,18 @@ def helper_program(g, core, T, topo):
     total = 0
     for t in range(R):
         for r in range(len(T.cores)):
-            h = helpers_of(T, topo, r, t)
-            if core not in h:
+            hs = helpers_of(T, topo, r, t)
+            if core not in hs:
                 continue
             src, dst = T.cores[r], T.cores[r ^ STEP[t]]
             n = len(topo.engines(src, core))
-            a, e = SHIP[h.index(core)]
-            g.wait_ge(T.sem["hc%d" % t], n)
-            total += send(g, T, topo, core, dst, T["lc%d" % t][:, a:e].bitcast(dt.uint8), T["rc%d" % t][:, a:e].bitcast(dt.uint8), "ac%d" % t)
-            g.wait_ge(T.sem["hs%d" % t], n)
-            total += send(g, T, topo, core, dst, T["ls%d" % t][:, a:e], T["rs%d" % t][:, a:e], "ac%d" % t)
-            if core == h[0]:
+            for h, (a, e) in enumerate(PART):
+                if hs[VIA[h]] == core:
+                    g.wait_ge(T.sem["hc%d_%d" % (t, h)], n)
+                    total += send(g, T, topo, core, dst, T["lc%d" % t][:, a:e].bitcast(dt.uint8), T["rc%d" % t][:, a:e].bitcast(dt.uint8), "ac%d" % t)
+                    g.wait_ge(T.sem["hs%d_%d" % (t, h)], n)
+                    total += send(g, T, topo, core, dst, T["ls%d" % t][:, a:e], T["rs%d" % t][:, a:e], "ac%d" % t)
+            if core == hs[0]:
                 g.wait_ge(T.sem["hl%d" % t], n)
                 total += send(g, T, topo, core, dst, T["ll%d" % t][:, 0:M], T["rl%d" % t][:, 0:M], "al%d" % t)
     if total:
@@ -245,6 +252,9 @@ def rank_program(g, core, T, topo):
     def scan(o, a, b, init, f0, f1):
         return op("v", lambda: g.vector.tensor_tensor_scan(o[0], a[0], b[0], ap(init), f0, f1), [o], [a, b, init])
 
+    def total(o, i):
+        return op("v", lambda: g.vector.tensor_reduce(o[0], i[0], AX.X, ALU.add), [o], [i])
+
     def mset(o, v):
         return op("v", lambda: g.vector.memset(o[0], v), [o], [])
 
@@ -269,7 +279,10 @@ def rank_program(g, core, T, topo):
     def col(k):
         return A("cols", k, k + 1)
 
-    QC, QM1, Q4, Q4M1, B4, PG, OFF, OFF16, OFF4 = [col(k) for k in (0, 1, 2, 6, 7, 8, 9, 10, 11)]
+    def bank(k, n):
+        return A("psd", 512 * k, 512 * k + n)
+
+    QC, QM1, Q4, Q4M1, B4, PG, OFF, OFF16, OFF4, OFFK, ENDK = [col(k) for k in (0, 1, 2, 6, 7, 8, 9, 10, 11, 16, 17)]
 
     def scan16(rowv, a=0, e=C, buf="ex16", ec="ec16"):
         scan(A(buf, a, e), rowv, A(ec, a, e), -B16, ALU.max, ALU.add)
@@ -280,13 +293,16 @@ def rank_program(g, core, T, topo):
     def list4(lst, a, e, buf):
         ts(lst, A(buf, a + 3, e, 4), 4.0, ALU.mult, OFF4, ALU.subtract)
 
+    def ends(a, e):
+        return A("ecx", 16 * a + 15, 16 * e, 16)
+
     def ship(t, h):
         mine = helpers_of(T, topo, rank, t)
         if mine:
-            a, e = SHIP[h]
-            rsend(mine[h], b8(A("rc%d" % t, a, e)), b8(A("qx%d" % t, a, e)), "hc%d" % t)
-            rsend(mine[h], A("rs%d" % t, a, e), A("sx%d" % t, a, e), "hs%d" % t)
-        elif h == len(SHIP) - 1:
+            a, e = PART[h]
+            rsend(mine[VIA[h]], b8(A("rc%d" % t, a, e)), b8(A("qx%d" % t, a, e)), "hc%d_%d" % (t, h))
+            rsend(mine[VIA[h]], A("rs%d" % t, a, e), A("sx%d" % t, a, e), "hs%d_%d" % (t, h))
+        elif h == len(PART) - 1:
             rsend(T.cores[rank ^ STEP[t]], b8(A("lc%d" % t)), b8(A("qx%d" % t)), "ac%d" % t)
             rsend(T.cores[rank ^ STEP[t]], A("ls%d" % t), A("sx%d" % t), "ac%d" % t)
 
@@ -296,211 +312,203 @@ def rank_program(g, core, T, topo):
         return A("fl", 4 * (AT[k] + a) + j, 4 * (AT[k] + e), 4)
 
     def pad(k):
-        return A("fl", 4 * (AT[k] + (16 * TILES[k][-1] if len(TILES[k]) == 4 else 0)), 4 * (AT[k] + WIDE[k]))
+        return 4 * (AT[k] + (16 * TILES[k][-1] if len(TILES[k]) == 4 else 0)), 4 * (AT[k] + WIDE[k])
+
+    def scores(t, part):
+        n = C if part else LOW
+        for o in ([A("psa", 0, C)] + [A("psb", 0, C)] * (t > 0) if part else [bank(0, LOW), bank(1, LOW)]):
+            mm(o, A("uq2"), A("us2"), A("qx%d" % t, 0, n), A("sx%d" % t, 0, n))
+
+    def own_mask(a, e):
+        tt(A("msk", a, e), A("psd" if e <= LOW else "psa", a, e), A("farq", a, e), ALU.add)
+
+    def own_scan(a, e):
+        scan(A("wsc", a, e), A("far0", a, e), A("msk", a, e), 0.0, ALU.add, ALU.min)
 
     dma("y", A("ut"), T.u[:])
-    tx1 = dma("s", A("x0", 2 * C, 4 * C), T.x[:, 2 * C:4 * C])
-    tx0 = dma("y", A("x0", 0, 2 * C), T.x[:, 0:2 * C])
-    wait("y", tx0)
-    wait("y", tx1)
+    first = [dma(e, A("x0", 4 * a, 4 * b), T.x[:, 4 * a:4 * b]) for e, (a, b) in zip("syy", PART)]
+    for tok in first:
+        wait("y", tok)
     dma("y", A("vt"), T.v[:])
     dma("y", b8(A("wq")), T.wc[:])
     dma("y", A("wp"), T.ws[:])
 
     iota(A("pc", 0, 5), [[-1, 5]], 16, 1)
     iota(A("s32"), [[1, 64]], 0)
+    iota(A("grp"), [[1, 8], [0, 16]], 1)
     iota(A("rr"), [[0, M], [1, 16]], 0)
-    iota(A("grp"), [[1, 8], [0, 64]], 1)
     iota(A("jm"), [[1, C]], -H)
     mset(A("ones"), 1.0)
+    op("g", lambda: g.affine_select(T.et[:], T.ones[:], [[-1, 516]], ALU.is_equal, 0.0, 3, 4), [A("et")], [A("ones")])
+    mset(A("fl", *pad(0)), 0.0)
     ts(A("pc", 5, 7), A("pc", 0, 2), 15, ALU.bitwise_and)
     ts(A("pc", 7, 12), A("pc", 0, 5), 2, ALU.logical_shift_right, 3, ALU.bitwise_and)
     ts(A("pc", 12, 13), A("pc", 0, 1), 3, ALU.bitwise_and)
     ts(A("pc", 13, 14), A("pc", 0, 1), 4, ALU.logical_shift_right)
+    mset(A("fl", *pad(1)), 0.0)
     ts(A("cu"), A("s32", 0, 8), 16.0, ALU.mult)
-    mset(pad(0), 0.0)
+    mset(A("acc", 0, 1), 0.0)
     cp(A("cols", 0, 9), A("pc", 5, 14))
-    for k in range(1, 5):
-        mset(pad(k), 0.0)
-    for k in range(5, len(TILES)):
-        n = 4 * WIDE[k] - (64 * TILES[k][-1] if len(TILES[k]) == 4 else 0)
-        act(pad(k), A("ones", 0, n), ACT.Copy, scale=0.0)
+    for k in (2, 3):
+        mset(A("fl", *pad(k)), 0.0)
+    for k in range(NT - 1, 3, -1):
+        a, e = pad(k)
+        act(A("fl", a, e), A("ones", 0, e - a), ACT.Copy, scale=0.0)
     r16 = A("s32", 0, 16)
     ts(A("pat", 0, 16), r16, QC, ALU.is_equal)
     ts(A("pat", 16, 32), r16, QM1, ALU.is_equal, -2.0, ALU.mult)
     ts(A("lq"), A("s32", 0, M), 0.0, ALU.mult, QC, ALU.add)
-    ts(A("farq"), A("rr"), QC, ALU.not_equal, FAR, ALU.mult)
-    tt(A("pat", 32, 48), A("pat", 0, 16), A("pat", 16, 32), ALU.add)
-    ts(A("far0"), A("rr"), 0.0, ALU.is_equal, FAR, ALU.mult)
-    act(A("ec16"), ind(A("pat", 32, 48), A("lq")), ACT.Copy, scale=B16)
+    for k in range(8):
+        ts(A("on", 512 * (k // 4) + k % 4, 512 * (k // 4 + 1), 4), A("grp"), PG, ALU.is_equal, -1.0 if k == 4 else 1.0, ALU.mult)
+        if k == 3:
+            tt(A("pat", 32, 48), A("pat", 0, 16), A("pat", 16, 32), ALU.add)
     act(col(12), QC, ACT.Sign)
-    act(col(13), A("pat", 47, 48), ACT.Identity, scale=B16, bias=QC)
-    act(OFF16, col(12), ACT.Identity, scale=2 * B16, bias=-B16 - H)
+    act(A("kp"), A("rr"), ACT.Sign)
     quant(A("uq"), A("us"), A("ut"))
-    ts(A("kp"), A("rr"), 0.0, ALU.not_equal)
+    quant(A("qx0", *PART[0]), A("sx0", *PART[0]), A("x0", 2 * LOW, 4 * LOW))
     op("v", lambda: g.vector.tensor_copy(T.uq2[:, 0:128].bitcast(dt.uint32), T.uq[:, 0:128].bitcast(dt.uint32).indirect(T.cu[:, 0:8])),
        [A("uq2")], [A("uq"), A("cu")])
     op("s", lambda: g.scalar.activation(T.us2[:, 0:128], T.us[:, 0:128].indirect(T.cu[:, 0:8]), ACT.Copy), [A("us2")], [A("us"), A("cu")])
-    quant(A("qx0", H, C), A("sx0", H, C), A("x0", 2 * C, 4 * C))
-    quant(A("qx0", 0, H), A("sx0", 0, H), A("x0", 0, 2 * C))
-    ts(A("on", 0, 512), A("grp"), PG, ALU.is_equal)
-    ts(A("on", 512, 1024), A("grp"), PG, ALU.is_equal)
-    act(A("ecx"), A("ec16"), ACT.Copy)
-    act(A("on", 512, 1024, 4), A("on", 0, 512, 4), ACT.Copy, scale=-1.0)
-    mset(A("acc", 0, 1), 0.0)
-    mset(A("endb", 0, 1), -1.0)
-    for h in range(len(SHIP)):
+    quant(A("qx0", *PART[1]), A("sx0", *PART[1]), A("x0", 0, 2 * LOW))
+    scores(0, 0)
+    ts(A("farq"), A("rr"), QC, ALU.not_equal, FAR, ALU.mult)
+    quant(A("qx0", LOW, C), A("sx0", LOW, C), A("x0", 4 * LOW, 4 * C))
+    scores(0, 1)
+    ts(A("far0"), A("rr"), 0.0, ALU.is_equal, FAR, ALU.mult)
+    act(A("ec16"), ind(A("pat", 32, 48), A("lq")), ACT.Copy, scale=B16)
+    act(col(13), A("pat", 47, 48), ACT.Identity, scale=B16, bias=QC)
+    act(OFF16, col(12), ACT.Identity, scale=2 * B16, bias=-B16 - H)
+    act(A("base", 0, M), A("jm", 0, C, 16), ACT.Identity, bias=col(13))
+    c1 = LOW - 64
+    own_mask(c1, LOW)
+    own_mask(0, c1)
+    own_scan(c1, LOW)
+    for h in range(len(PART)):
         ship(0, h)
+
+    def unpacker(b):
+        quant(A("eq", 128 * b, 128 * b + 128), A("es", 128 * b, 128 * b + 128), A("et", 3 - b, 515 - b))
+
+    spare = [[[lambda b=b: unpacker(b)] for b in range(4)]
+             + [[lambda: ts(A("r4"), r16, 3, ALU.bitwise_and), lambda: ts(A("kc", 0, 4), A("s32", 0, 4), 16.0, ALU.mult, QC, ALU.add),
+                 lambda: mset(A("ww", 0, 1), 0.0)],
+                [lambda: ts(A("pat", 48, 64), A("r4"), Q4, ALU.is_equal), lambda: ts(A("pat", 64, 80), A("r4"), Q4M1, ALU.is_equal, -2.0, ALU.mult),
+                 lambda: tt(A("ec2", 15, S, 16), A("ec2", 15, S, 16), A("kc", 0, 4), ALU.subtract)],
+                [lambda: tt(A("pat", 80, 96), A("pat", 48, 64), A("pat", 64, 80), ALU.add), lambda: mset(A("se"), 0.0)]],
+             [[lambda: quant(A("vq"), A("vs"), A("vt"))]]]
 
     for t in range(R):
         partner = T.cores[rank ^ STEP[t]]
         mine = helpers_of(T, topo, rank, t)
         theirs = helpers_of(T, topo, rank ^ STEP[t], t)
-        qx, sx = "qx%d" % t, "sx%d" % t
         li, ll, lc, ls = "li%d" % t, "ll%d" % t, "lc%d" % t, "ls%d" % t
         qz, sz, qf, sf = "qz%d" % t, "sz%d" % t, "qf%d" % t, "sf%d" % t
+        arrive("ac%d" % t, sum(2 * len(topo.engines(k, core)) for k in ([theirs[v] for v in VIA] if theirs else [partner])), [A(lc), A(ls)])
+        arrive("al%d" % t, len(topo.engines(theirs[0] if theirs else partner, core)), [A(ll, 0, M)])
 
-        mm(A("psa", 0, C), A("uq2"), A("us2"), A(qx), A(sx))
-        mm(A("psb", 0, C), A("uq2"), A("us2"), A(qx), A(sx))
-        srcs = theirs if theirs else [partner]
-        arrive("ac%d" % t, sum(2 * len(topo.engines(k, core)) for k in srcs), [A(lc), A(ls)])
-        arrive("al%d" % t, len(topo.engines(srcs[0], core)), [A(ll, 0, M)])
-        if t == 0:
-            op("g", lambda: g.affine_select(T.et[:], T.ones[:], [[-1, 516]], ALU.is_equal, 0.0, 3, 4), [A("et")], [A("ones")])
+        ns, nv = (NS + 1, 2 * NV) if t else (NS, NV)
+        turns = list(range(NS - 1, NS - 6, -1)) + list(range(NS, ns + 1)) + list(range(NS - 6, nv, -1))
+        done = [0]
 
-        def own_mask(a, e):
-            tt(A("msk", a, e), A("psa", a, e), A("farq", a, e), ALU.add)
+        def s_first(k):
+            m, o = turns[k], (k % 3) * C
+            act(A("sfl", o, o + 16 * m), bank(1, 16 * m) if m <= NS else A("psb", 0, 16 * m), ACT.Sign, scale=-1.0, bias=A("wsc", 16 * m + 15, 16 * m + 16))
 
-        def own_scan(a, e):
-            scan(A("wsc", a, e), A("far0", a, e), A("msk", a, e), 0.0, ALU.add, ALU.min)
-
-        def own(m):
-            return A("wsc", 16 * m + 15, 16 * m + 16)
-
-        def s_first(m):
-            o = (m % 3) * C
-            act(A("sfl", o, o + 16 * m), A("psb", 0, 16 * m), ACT.Sign, scale=-1.0, bias=own(m))
-
-        def s_second(m):
-            o = (m % 3) * C
+        def s_second(k):
+            m, o = turns[k], (k % 3) * C
             act(flags(m), A("sfl", o, o + 16 * m), ACT.Relu, acc=A("acc", m, m + 1))
 
-        def s_tile(k):
-            for m in TILES[k]:
-                if m > 1:
-                    s_first(m - 1)
-                s_second(m)
+        def s_blocks(n):
+            for k in range(done[0], done[0] + n):
+                if k + 1 < len(turns):
+                    s_first(k + 1)
+                s_second(k)
+            done[0] += n
 
         def v_first(m):
-            ts(flags(m), A("psa", 0, 16 * m), own(m), ALU.is_lt)
+            ts(flags(m), A("psa" if m > NS else "psd", 0, 16 * m), A("wsc", 16 * m + 15, 16 * m + 16), ALU.is_lt)
 
         def v_second(m):
-            e = H * (m - NS)
-            scan(A("res", e - 8 * m, e), flags(m, 0, 8 * m), flags(m, 8 * m), 0.0, ALU.add, ALU.add)
+            if m > NS:
+                e = H * (m - ns)
+                scan(A("res", e - 8 * m, e), flags(m, 0, 8 * m), flags(m, 8 * m), 0.0, ALU.add, ALU.add)
+            else:
+                total(A("acc", m, m + 1), flags(m))
 
-        def pack(k):
-            a, e = AT[k], AT[k] + WIDE[k]
-            quant(A(qf, a, e), A(sf, a, e), A("fl", 4 * a, 4 * e))
-
-        def total(k, start=False, stop=False):
+        def pack(k, start=False, stop=False):
             a, e, o = AT[k], AT[k] + WIDE[k], 0 if k else 128
+            quant(A(qf, a, e), A(sf, a, e), A("fl", 4 * a, 4 * e))
             mm(A("pse", 0, e - a), A("oq", o, o + 128), A("op", o, o + 128), A(qf, a, e), A(sf, a, e), start, stop)
 
-        c1, c2 = 16 * (NS - 4), 16 * (NS + 1)
-        own_mask(c1, c2)
-        own_mask(c2, C)
-        own_scan(c1, c2)
-        own_mask(0, c1)
-        own_scan(c2, C)
-        s_first(NS)
-        s_tile(2)
+        s_first(0)
+        s_blocks(3)
         own_scan(0, c1)
-        v_first(M - 1)
-        v_first(M - 2)
-        tt(flags(0), A("psa", 0, C), A("wsc"), ALU.is_gt)
-        v_first(M - 3)
         if t == 0:
             quant(A("oq"), A("op"), A("on"))
-            ts(A("base", 0, M), A("jm", 0, C, 16), col(13), ALU.add)
+        tt(flags(0, 0, LOW), bank(0, LOW), A("wsc", 0, LOW), ALU.is_gt)
+        for m in range(nv, 0, -1):
+            v_first(m)
+        own_mask(LOW, C)
+        scan(A("cor", 0, LOW), A("kp", 0, LOW), flags(0, 0, LOW), 0.0, ALU.mult, ALU.add)
+        for m in range(1, NV + 1):
+            v_second(m)
+        own_scan(LOW, C)
+        for m in range(NV + 1, nv + 1):
+            v_second(m)
+        s_blocks(len(turns) - 3)
+        if t == 0:
+            cp(A("ecx"), A("ec16"))
+        v_first(M - 1)
+        v_first(M - 2)
+        tt(flags(0, LOW), A("psa", LOW, C), A("wsc", LOW, C), ALU.is_gt)
+        v_first(M - 3)
         v_second(M - 1)
-        pack(0)
-        total(0, start=True)
-        s_tile(3)
+        v_second(M - 2)
+        scan(A("cor", LOW, C), A("kp", LOW, C), flags(0, LOW), 0.0, ALU.mult, ALU.add)
+        pack(0, start=True)
         v_first(M - 4)
         pack(2)
-        total(2)
         v_first(M - 5)
-        scan(A("cor"), A("kp"), flags(0), 0.0, ALU.mult, ALU.add)
         v_first(M - 6)
-        s_tile(4)
         pack(3)
-        total(3)
-        v_first(M - 7)
+        if ns < M - 7:
+            v_first(M - 7)
         tt(A("t1", 0, M), A("base", 0, M), A("cor", 15, C, 16), ALU.add)
-        v_second(M - 2)
-        pack(1)
-        total(1)
-        s_tile(5)
-        pack(4)
-        total(4)
-        s_tile(6)
-        v_second(M - 3)
-        v_second(M - 4)
-        pack(5)
-        total(5)
-        v_second(M - 5)
         pack(6)
-        total(6, stop=True)
-        v_second(M - 6)
-        v_second(M - 7)
-        tt(A("ecx", 15, c2, 16), A("t1", 0, NS + 1), A("acc", 0, NS + 1), ALU.subtract)
-        tt(A("ecx", c2 + 15, C, 16), A("t1", NS + 1, M), A("res", H - 1, H * (M - 1 - NS), H), ALU.subtract)
+        v_second(M - 3)
+        pack(1)
+        pack(4)
+        for m in range(M - 4, ns + 1, -1):
+            v_second(m)
+        pack(5, stop=True)
+        v_second(ns + 1)
+        tt(ends(0, ns + 1), A("t1", 0, ns + 1), A("acc", 0, ns + 1), ALU.subtract)
+        tt(ends(ns + 1, M), A("t1", ns + 1, M), A("res", H - 1, H * (M - 1 - ns), H), ALU.subtract)
         scan16(A("pse", 0, C), ec="ecx")
         list16(A(li, 0, M))
-        if mine:
-            rsend(mine[0], A("rl%d" % t, 0, M), A(li, 0, M), "hl%d" % t)
-        else:
-            rsend(partner, A(ll, 0, M), A(li, 0, M), "al%d" % t)
+        rsend(mine[0] if mine else partner, A("rl%d" % t if mine else ll, 0, M), A(li, 0, M), ("hl%d" if mine else "al%d") % t)
 
         scatter(A("orow"), A(li, 0, M), A("jm"))
         if t == 0:
             iota(A("p1024"), [[int(KW), C]], 0)
-            iota(A("c2"), [[int(KW), C]], -int(KW))
-            for b in range(4):
-                quant(A("eq", 128 * b, 128 * b + 128), A("es", 128 * b, 128 * b + 128), A("et", 3 - b, 515 - b))
-            ts(A("r4"), r16, 3, ALU.bitwise_and)
-            ts(A("kc", 4, 8), A("s32", 0, 4), 16.0, ALU.mult, QC, ALU.add)
-            ts(A("pat", 48, 64), A("r4"), Q4, ALU.is_equal)
-            ts(A("pat", 64, 80), A("r4"), Q4M1, ALU.is_equal, -2.0, ALU.mult)
-            act(A("ec"), A("ec16", 0, S), ACT.Copy, scale=BIG / B16)
-            act(A("kc", 0, 4), A("kc", 4, 8), ACT.Identity, bias=-0.5)
+            act(A("eck"), A("ec16"), ACT.Copy, scale=BIG / B16)
+            act(A("ec2"), A("ec16", 0, S), ACT.Copy, scale=BIG / B16)
             act(OFF, col(12), ACT.Identity, scale=2 * BIG, bias=-BIG)
+            act(OFFK, col(12), ACT.Identity, scale=2 * BIG, bias=-BIG - KW)
             act(col(14), Q4, ACT.Sign)
             act(col(15), B4, ACT.Identity, scale=-1.0, bias=-4 * (B16 + H))
+            act(ENDK, A("pat", 47, 48), ACT.Identity, scale=B16, bias=OFFK)
             act(OFF4, col(14), ACT.Identity, scale=8 * B16, bias=col(15))
-        else:
-            quant(A("vq"), A("vs"), A("vt"))
-        for b in range(4):
-            mm(A("psd", 512 * b, 512 * b + C), A("eq", 128 * b, 128 * b + 128), A("es", 128 * b, 128 * b + 128), A(lc), A(ls))
-
-        def unpack(b):
-            act(A("dp", b, 4 * C, 4), A("psd", 512 * b, 512 * b + C), ACT.Copy)
-
-        if t:
-            for b in range(4):
-                unpack(b)
 
         tb_, kb_, bb_ = ["ta", "tb"], ["ka", "kb"], ["ba", "bb"]
         halves = [(0, MA), (MA, M)]
-        for c, e in halves:
-            act(A("tp", 16 * c, 16 * e), ind(A("orow"), A(ll, c, e)), ACT.Copy)
-        for c, e in halves:
-            ts(A("ka", 16 * c, 16 * e), ind(A("orow"), A(ll, c, e)), KW, ALU.mult, KW * H + 1.0, ALU.add)
-        for c, e in halves:
-            scan16(A("tp", 16 * c, 16 * e), 16 * c, 16 * e)
-        for c, e in halves:
-            list16(A("lt", c, e), 16 * c, 16 * e)
+        act(A("tp", HA, C), ind(A("orow"), A(ll, MA, M)), ACT.Copy)
+        cp(A("tp", 0, HA), ind(A("orow"), A(ll, 0, MA)))
+        scan16(A("tp"))
         act(A("ba"), A("tp"), ACT.Identity, scale=KW, bias=KW * H + 2.0)
+        ts(A("ka", 0, HA), A("tp", 0, HA), KW, ALU.mult, KW * H + 1.0, ALU.add)
+        list16(A("lt", 0, M))
+        ts(A("ka", HA, C), A("tp", HA, C), KW, ALU.mult, KW * H + 1.0, ALU.add)
         for k in range(DBL - 1):
             a, b = k % 2, (k + 1) % 2
             for c, e in halves:
@@ -510,54 +518,74 @@ def rank_program(g, core, T, topo):
             for c, e in halves:
                 scan16(A(tb_[b], 16 * c, 16 * e), 16 * c, 16 * e)
             for c, e in halves:
+                if c and k < len(spare[t]):
+                    for f in spare[t][k]:
+                        f()
                 list16(A("lt", (k + 1) * M + c, (k + 1) * M + e), 16 * c, 16 * e)
             for c, e in halves:
                 act(A(bb_[b], 16 * c, 16 * e), A(kb_[b], 16 * c, 16 * e), ACT.Identity, bias=float(2 ** (k + 1)))
+        for b in range(4):
+            mm(bank(b, C), A("eq", 128 * b, 128 * b + 128), A("es", 128 * b, 128 * b + 128), A(lc), A(ls))
 
         k = DBL - 1
         kn = kb_[DBL % 2]
-        HA = 16 * MA
+
+        def leaders(a, e):
+            scan(A("yy", a, e), A(kn, a, e), A("p1024", a, e), 0.0, ALU.max, ALU.max)
+
+        def cycle_ends(a, e):
+            scan(A("ww", 1 + a, 1 + e), A("yy", a, e), A("p1024", a, e), A("ww", a, a + 1), ALU.add, ALU.subtract)
+
+        def keys(a, e):
+            scan(A("exk", a, e), A(kn, a, e), A("eck", a, e), -BIG, ALU.max, ALU.add)
+
+        def members(a, e):
+            ts(A("lm", a, e), A("exk", 16 * a + 15, 16 * e, 16), OFFK, ALU.subtract, 1.0 / KW, ALU.mult)
+
+        def leader_key(a, e):
+            ts(A("t2", a, e), A("lm", a, e), KW, ALU.mult, ENDK, ALU.add)
+
+        def steps(a, e):
+            tt(ends(a, e), A("t2", a, e), A("exk", 16 * a + 15, 16 * e, 16), ALU.subtract)
+
         for c, e in halves:
             tt(A(kn, 16 * c, 16 * e), ind(A(bb_[k % 2]), A("lt", k * M + c, k * M + e)), A(kb_[k % 2], 16 * c, 16 * e), ALU.min)
-            act(A("mrow", 16 * c, 16 * e), A(kn, 16 * c, 16 * e), ACT.Identity, scale=1.0 / KW, bias=-float(H))
-        for c, e in halves:
-            scan(A("yy", 16 * c, 16 * e), A(kn, 16 * c, 16 * e), A("p1024", 16 * c, 16 * e), 0.0, ALU.max, ALU.max)
-        scan(A("ww", 0, HA), A("yy", 0, HA), A("c2", 0, HA), -KW - H, ALU.add, ALU.subtract)
-        scan16(A("mrow", 0, HA), 0, HA)
-        scan(A("endb", 1, S + 1), A("yy", 0, S), A("p1024", 0, S), -1.0, ALU.add, ALU.subtract)
-        scan(A("ww", HA, C), A("yy", HA, C), A("c2", HA, C), A("ww", HA - 1, HA), ALU.add, ALU.subtract)
-        list16(A("lm", 0, MA), 0, HA)
-        scan16(A("mrow", HA, C), HA, C)
-        for m in range(4):
-            act(A("sj", S * m, S * m + S), A("endb", 1, S + 1), ACT.Sign, scale=-1.0, bias=A("kc", m, m + 1), acc=A("cc", m, m + 1))
-        tt(A("se"), A("endb", 0, S), A("endb", 1, S + 1), ALU.add)
-        if t == 0:
-            tt(A("pat", 80, 96), A("pat", 48, 64), A("pat", 64, 80), ALU.add)
-            ts(A("zz"), A("rr", 0, S), QC, ALU.is_equal)
-        tt(A("posr", 0, HA), ind(A("ww"), A("lm", 0, MA)), A(kn, 0, HA), ALU.subtract)
-        list16(A("lm", MA, M), HA, C)
         if t == 0:
             act(A("ec4"), ind(A("pat", 80, 96), A("lq")), ACT.Copy, scale=B16)
-            tt(A("zz"), A("zz"), A("s32"), ALU.mult)
-        ts(A("lcc", 0, 4), A("cc", 0, 4), float(S), ALU.add, 0.5, ALU.mult)
-        scan16(A("posr", 0, HA), 0, HA)
-        tt(A("posr", HA, C), ind(A("ww"), A("lm", MA, M)), A(kn, HA, C), ALU.subtract)
-        act(A("seg"), ind(A("se"), A("lcc", 0, 4)), ACT.Identity, bias=1.0)
-        if t == 0:
-            tt(A("ec2"), A("ec"), A("zz"), ALU.subtract)
-            for b in range(4):
-                unpack(b)
-        list16(A("lp", 0, MA), 0, HA)
-        scan16(A("posr", HA, C), HA, C)
+        leaders(0, HA)
+        keys(0, HA)
+        cycle_ends(0, HA)
+        leaders(HA, C)
+        for m in range(4):
+            act(A("sj", 65 * m, 65 * m + 65), A("ww", 0, S + 1), ACT.Sign, scale=-1.0, bias=A("kc", m, m + 1), acc=A("cc", m, m + 1))
+        act(A("se", 1, 2 * S + 2, 2), A("ww", 0, S + 1), ACT.Copy, scale=2.0)
+        keys(HA, C)
+        members(0, MA)
+        cycle_ends(HA, C)
+        members(MA, M)
+        leader_key(0, MA)
+        act(A("posr", 0, HA), ind(A("ww", 0, C + 1), A("lm", 0, MA)), ACT.Identity, bias=-float(H))
+        scan(A("se", 2, 2 * S + 2, 2), A("ww", 0, S), A("ww", 1, S + 1), 0.0, ALU.min, ALU.add)
+        ts(A("lcc", 0, 4), A("cc", 0, 4), float(S + 1), ALU.add)
+        leader_key(MA, M)
+        steps(0, MA)
+        ts(A("posr", HA, C), ind(A("ww", 0, C + 1), A("lm", MA, M)), float(H), ALU.subtract)
+        act(A("seg"), ind(A("se"), A("lcc", 0, 4)), ACT.Copy)
+        for b in range(4):
+            act(A("dp", b, 4 * C, 4), bank(b, C), ACT.Copy)
+        steps(MA, M)
+        scan16(A("posr", 0, HA), 0, HA, ec="ecx")
+        scan16(A("posr", HA, C), HA, C, ec="ecx")
         scan(A("ex2"), A("seg"), A("ec2"), -BIG, ALU.max, ALU.add)
+        list16(A("lp", 0, MA), 0, HA)
         list16(A("lp", MA, M), HA, C)
         ts(A("lk", 0, 4), A("ex2", 15, S, 16), OFF, ALU.subtract)
         scatter(A("erow"), A("lp"), A("jm"))
 
-        banks = [[A("psd", 512 * b, 512 * b + PART[h][1] - PART[h][0]) for b in range(4)] for h in (0, 2)]
-        ybank = ("psa", "psb", "pse", "psf")
-        banks.insert(1, [A(n, 0, PART[1][1] - PART[1][0]) for n in ybank])
+        banks = [[bank(b, PART[h][1] - PART[h][0]) for b in range(4)] for h in (0, 1)]
+        banks.append([A(n, 0, C - LOW) for n in ("psa", "psb", "pse", "psf")])
         xo, xn, nx, ns_ = "x%d" % t, "x%d" % (t + 1), "qx%d" % (t + 1), "sx%d" % (t + 1)
+        outs = [None, (0, LOW), (LOW, C)]
 
         def run(name, h):
             return A(name, 4 * PART[h][0], 4 * PART[h][1])
@@ -577,36 +605,48 @@ def rank_program(g, core, T, topo):
         def own_s(a, e):
             act(A("z", 4 * a, 4 * e), ind(A(xo), A("le", a // 4, e // 4)), ACT.Copy)
 
-        def layer(h):
+        def products(h, bs):
+            a, e = PART[h]
+            for b in bs:
+                mm(banks[h][b], A("wq", 128 * b, 128 * b + 128), A("wp", 128 * b, 128 * b + 128), A(qz, a, e), A(sz, a, e))
+
+        def layer(h, bs=range(4)):
             a, e = PART[h]
             quant(A(qz, a, e), A(sz, a, e), run("z", h))
-            for b in range(4):
-                mm(banks[h][b], A("wq", 128 * b, 128 * b + 128), A("wp", 128 * b, 128 * b + 128), A(qz, a, e), A(sz, a, e))
+            products(h, bs)
 
         def finish(h):
             a, e = PART[h]
             quant(A(nx, a, e), A(ns_, a, e), run(xn, h))
-            if t == R - 1:
-                mm(A(ybank[h], 0, e - a), A("vq"), A("vs"), A(nx, a, e), A(ns_, a, e))
-                dma("y", T.oc[:, 4 * a:4 * e], b8(A(nx, a, e)))
+            if t < R - 1:
+                if h:
+                    scores(t + 1, h - 1)
+                ship(t + 1, h)
             elif h:
-                ship(t + 1, h - 1)
+                a, e = outs[h]
+                mm(bank(h, e - a), A("vq"), A("vs"), A(nx, a, e), A(ns_, a, e))
+                dma("y", T.oc[:, 4 * a:4 * e], b8(A(nx, a, e)))
 
         def store(h):
-            if t == R - 1:
-                a, e = PART[h]
-                act(A("ybuf", a, e), A(ybank[h], 0, e - a), ACT.Copy)
-                dma("s", T.y[:, a:e], A("ybuf", a, e))
+            a, e = outs[h]
+            act(A("ybuf", a, e), bank(h, e - a), ACT.Copy)
+            dma("s", T.y[:, a:e], A("ybuf", a, e))
 
-        def up_v(h):
-            ts(run("z64", h), run("z", h), 64.0, ALU.mult)
+        def scales(e, ks):
+            for k in ks:
+                dma(e, T.osc[4 * k:4 * k + 4, :], (T[ns_][32 * k:32 * k + 4, :], A(ns_)[1]))
 
-        def up_s(h):
-            act(run("z64", h), run("z", h), ACT.Copy, scale=64.0)
+        def up_v(h, bs=None):
+            for o, i in ([(run("z64", h), run("z", h))] if bs is None else [(tile("z64", h, b), tile("z", h, b)) for b in bs]):
+                ts(o, i, 64.0, ALU.mult)
 
-        def down_v(h, bs=None):
-            for o, i in ([(run(xn, h), run("xs", h))] if bs is None else [(tile(xn, h, b), tile("xs", h, b)) for b in bs]):
-                ts(o, i, 1.0 / 64.0, ALU.mult)
+        def up_s(h, bs):
+            for b in bs:
+                act(tile("z64", h, b), tile("z", h, b), ACT.Copy, scale=64.0)
+
+        def down_v(h, bs):
+            for b in bs:
+                ts(tile(xn, h, b), tile("xs", h, b), 1.0 / 64.0, ALU.mult)
 
         def down_s(h, bs):
             for b in bs:
@@ -616,61 +656,67 @@ def rank_program(g, core, T, topo):
             for b in bs:
                 tt(tile("xs", h, b), banks[h][b], tile("z64", h, b), ALU.add)
 
-        a0, a1 = PART[0][0], PART[1][0]
-        mid = (a0 + C) // 2
-        words(a0, C)
-        act(A("e2r"), ind(A("erow"), A("lk", 0, 4)), ACT.Copy)
+        a0, mid = PART[0][0], (PART[0][0] + LOW) // 2
+        words(a0, LOW)
+        act(A("e3r"), ind(A("erow"), A("lk", 0, 4)), ACT.Copy)
         words(S, a0)
-        offsets(a0, C)
+        offsets(a0, LOW)
         offsets(S, a0)
-        own_s(mid, C)
-        own_v(a0, mid)
-        scan16(A("e2r"), 0, S, "ex17")
-        own_s(a1, a1 + 72)
-        layer(0)
-        list16(A("le2", 0, 4), 0, S, "ex17")
-        up_v(0)
-        act(A("e3r"), ind(A("tp"), A("le2", 0, 4)), ACT.Copy)
-        own_s(a1 + 72, a0)
-        add(0, (0, 1))
         scan16(A("e3r"), 0, S, "ex17", "ec4")
-        add(0, (2, 3))
+        own_s(mid, LOW)
+        own_v(a0, mid)
+        words(LOW, C)
         list4(A("le3"), 0, S, "ex17")
-        layer(1)
-        own_s(S, a1)
+        own_s(S, a0)
         act(A("z", 0, 4 * S), ind(A("dp"), A("le3")), ACT.Copy)
-        up_v(1)
-        down_v(0)
-        add(1, (0, 1))
-        finish(0)
+        layer(0)
+        offsets(LOW, C)
+        up_v(0)
+        own_s(LOW, LOW + 64)
+        add(0, (0, 1))
+        layer(1, (0, 1))
+        up_s(1, (2, 3))
+        own_s(LOW + 64, C)
+        add(0, (2,))
+        products(1, (2,))
+        up_v(1, (0, 1))
+        add(0, (3,))
+        products(1, (3,))
+        down_v(0, (0, 1))
+        down_s(0, (2, 3))
+        add(1)
         layer(2)
-        add(1, (2, 3))
-        up_v(2)
-        down_s(1, range(4))
-        add(2, (0, 1))
+        down_s(1, (0, 2))
+        down_v(1, (1, 3))
+        up_s(2, range(4))
+        finish(0)
         finish(1)
-        store(0)
-        add(2, (2, 3))
-        down_s(2, (0, 1))
-        down_v(2, (2, 3))
+        add(2)
         if t == R - 1:
             act(A("elf"), A("erow"), ACT.Identity, bias=float(H))
             dma("y", T.el[:], (T.elf[0:128:16, :], A("elf")[1]))
-        store(1)
-        finish(2)
-        store(2)
-
-    sx = "sx%d" % R
-    for k in range(4):
-        dma("y", T.osc[4 * k:4 * k + 4, :], (T[sx][32 * k:32 * k + 4, :], A(sx)[1]))
+            down_s(2, (2,))
+            store(1)
+            down_v(2, (0, 1, 3))
+            finish(2)
+            scales("s", (0, 1))
+            scales("y", (2, 3))
+            store(2)
+        else:
+            down_v(2, (0, 1))
+            down_s(2, (2, 3))
+            own_mask(c1, LOW)
+            own_mask(0, c1)
+            own_scan(c1, LOW)
+            finish(2)
 
     g.wait_ge(T.sem["sent"], nsent[0])
-    done = set()
-    ends = []
+    seen = set()
+    final = []
     for sem in reversed(order):
-        if sem not in done:
-            done.add(sem)
-            ends.append(sem)
-    for sem in reversed(ends):
+        if sem not in seen:
+            seen.add(sem)
+            final.append(sem)
+    for sem in reversed(final):
         if waited.get(sem, 0) < count[sem]:
             g.wait_ge(T.sem[sem], count[sem])

from concourse.mybir import dt, AluOpType as ALU, ActivationFunctionType as ACT, AxisListType as AX

C, S, R = 416, 64, 2
STEP = [4, 1]
M = C // 16
H = C // 2
NS = 18
NV = 2
BIG = float(2 ** 21)
B16 = 512.0
FAR = float(2 ** 90)
KW = 2048.0
DBL = 9
MA = 14
HA = 16 * MA
LOW = 16 * NS
PART = [(LOW // 2, LOW), (0, LOW // 2), (LOW, C)]
VIA = [1, 0, 1]

TILES = [[0] + list(range(M - 1, M - 4, -1))] + [list(range(m, max(m - 4, 0), -1)) for m in range(M - 4, 0, -4)]
WIDE = [C] + [max(16 * t[0], 128) for t in TILES[1:]]
NT = len(TILES)
AT = [sum(WIDE[:k]) for k in range(NT)]
SLOT = {m: (k, j) for k, t in enumerate(TILES) for j, m in enumerate(t)}

F32, BF, F16, U16, I32, X4, U8 = "float32", "bfloat16", "float16", "uint16", "int32", "float8_e4m3fn_x4", "uint8"
SCRATCH = {}


def _decl(dtype, cols, names, where="sbuf"):
    for n in names.split():
        SCRATCH[n] = (where, [128, cols], dtype)


_decl(BF, 4 * C, "x0 x1 x2 z xs z64 dp")
_decl(BF, 512, "ut vt")
_decl(BF, 516, "ones et")
_decl(BF, 1024, "on")
_decl(BF, 4 * sum(WIDE), "fl")
_decl(X4, sum(WIDE), "qf0 qf1")
_decl(U8, sum(WIDE), "sf0 sf1")
_decl(X4, C, "qx0 qx1 qx2 qz0 qz1 lc0 lc1 rc0 rc1")
_decl(U8, C, "sx0 sx1 sx2 sz0 sz1 ls0 ls1 rs0 rs1")
_decl(X4, 128, "uq uq2 vq")
_decl(U8, 128, "us us2 vs")
_decl(X4, 256, "oq")
_decl(U8, 256, "op")
_decl(X4, 512, "wq eq")
_decl(U8, 512, "wp es")
_decl(U16, 32, "li0 li1 ll0 ll1 rl0 rl1")
_decl(U16, M, "lm lp lq")
_decl(U16, C // 4, "le")
_decl(U16, M * DBL, "lt")
_decl(U16, 8, "cu lk lcc")
_decl(U16, S // 4, "le3")
_decl(F32, C, "p1024 msk wsc exk ka kb ba bb yy elf ybuf")
_decl(BF, C, "jm rr far0 farq kp ec16 ec4 eck ta tb tp orow posr erow")
_decl(F16, C, "ex16 ex4 ecx cor")
_decl(F16, S, "ex17")
_decl(F16, H * (M - 1 - NS), "res")
_decl(BF, C * 3, "sfl")
_decl(BF, 128, "pat grp")
_decl(F32, 32, "acc t1 t2 base cols kc cc")
_decl(I32, 64, "s32")
_decl(I32, 16, "pc r4")
_decl(F32, C + 8, "ww")
_decl(F32, S, "seg ex2 ec2")
_decl(F32, 2 * S + 8, "se")
_decl(F32, 4 * S + 8, "sj")
_decl(BF, S, "e3r")
_decl(F32, 512, "psa psb pse psf", "psum")
_decl(F32, 2048, "psd", "psum")

POOL = {"v": 48, "s": 32, "t": 12, "g": 10}
SEMAPHORES = [e + str(k) for e in POOL for k in range(POOL[e])]
SEMAPHORES += ["d%d" % k for k in range(20)]
SEMAPHORES += ["sent"] + [n + str(t) for t in range(R) for n in ("ac", "al", "hl")]
SEMAPHORES += ["%s%d_%d" % (n, t, h) for t in range(R) for n in ("hc", "hs") for h in range(len(PART))]


def helpers_of(T, topo, r, t):
    src, dst = T.cores[r], T.cores[r ^ STEP[t]]
    if topo.may_write(src, dst):
        return []
    c = [k for k in topo.cores_of(src) if T.rank_of(k) is None and topo.may_write(k, dst)]
    c.sort(key=lambda k: topo.die(k) != topo.die(src))
    return c[:max(VIA) + 1]


def send(g, T, topo, src, dst, out_ap, in_ap, sem):
    rid, pid = topo.addr(dst, src)
    g.remote_dma(out_ap, in_ap, T.sem[sem], T.sem["sent"], pid, rid, topo.mask(src, dst))
    return len(topo.engines(src, dst))


def helper_program(g, core, T, topo):
    total = 0
    for t in range(R):
        for r in range(len(T.cores)):
            hs = helpers_of(T, topo, r, t)
            if core not in hs:
                continue
            src, dst = T.cores[r], T.cores[r ^ STEP[t]]
            n = len(topo.engines(src, core))
            for h, (a, e) in enumerate(PART):
                if hs[VIA[h]] == core:
                    g.wait_ge(T.sem["hc%d_%d" % (t, h)], n)
                    total += send(g, T, topo, core, dst, T["lc%d" % t][:, a:e].bitcast(dt.uint8), T["rc%d" % t][:, a:e].bitcast(dt.uint8), "ac%d" % t)
                    g.wait_ge(T.sem["hs%d_%d" % (t, h)], n)
                    total += send(g, T, topo, core, dst, T["ls%d" % t][:, a:e], T["rs%d" % t][:, a:e], "ac%d" % t)
            if core == hs[0]:
                g.wait_ge(T.sem["hl%d" % t], n)
                total += send(g, T, topo, core, dst, T["ll%d" % t][:, 0:M], T["rl%d" % t][:, 0:M], "al%d" % t)
    if total:
        g.wait_ge(T.sem["sent"], total)


def rank_program(g, core, T, topo):
    rank = T.rank_of(core)
    if rank is None:
        helper_program(g, core, T, topo)
        return

    Q = {"v": g.vector, "s": g.scalar, "t": g.tensor, "g": g, "y": g.sync}
    known = {e: {} for e in Q}
    count = {}
    waited = {}
    last = {}
    order = []
    turn = {e: 0 for e in POOL}
    ndma = [0]
    nsent = [0]
    hist = {}

    def wait(e, tok):
        sem, val, seen = tok
        if known[e].get(sem, 0) >= val:
            return
        Q[e].wait_ge(T.sem[sem], val)
        waited[sem] = max(waited.get(sem, 0), val)
        k = known[e]
        for s2 in seen:
            if k.get(s2, 0) < seen[s2]:
                k[s2] = seen[s2]
        k[sem] = val

    def A(name, a=0, b=None, s=1):
        n = SCRATCH[name][1][1]
        b = n if b is None else b
        m = 0
        if SCRATCH[name][0] == "psum":
            m = 1 << (a // 512)
        elif s == 1:
            m = ((1 << (b - a)) - 1) << a
        else:
            for j in range(a, b, s):
                m |= 1 << j
        ap = T[name][:, a:b] if s == 1 else T[name][:, a:b:s]
        return (ap, [(name, m)])

    def ind(win, off):
        return (win[0].indirect(off[0]), win[1] + off[1])

    def before(e, reads, writes):
        need = []
        for name, m in reads:
            ps = SCRATCH[name][0] == "psum"
            for m2, tok, e2, w in hist.get(name, []):
                if m & m2 and (w or (ps and e2 != e)):
                    need.append(tok)
        for name, m in writes:
            for m2, tok, e2, w in hist.get(name, []):
                if m & m2:
                    need.append(tok)
        need.sort(key=lambda k: -sum(k[2].values()))
        for tok in need:
            wait(e, tok)

    def after(e, reads, writes, tok):
        for name, m in writes:
            hist[name] = [h for h in hist.get(name, []) if h[0] & ~m] + [(m, tok, e, True)]
        for name, m in reads:
            hist.setdefault(name, []).append((m, tok, e, False))

    def regs(xs):
        out = []
        for x in xs:
            if isinstance(x, tuple):
                out += x[1]
        return out

    def ap(x):
        return x[0] if isinstance(x, tuple) else x

    def token(e, sem, n):
        count[sem] = count.get(sem, 0) + n
        tok = (sem, count[sem], dict(known[e]))
        last[sem] = tok
        order.append(sem)
        return tok

    def op(e, fn, outs, ins, adds=False):
        reads, writes = regs(ins), regs(outs)
        before(e, reads, [] if adds else writes)
        sem = e + str(turn[e] % POOL[e])
        turn[e] += 1
        if sem in last:
            wait(e, last[sem])
        fn().then_inc(T.sem[sem], 1)
        tok = token(e, sem, 1)
        after(e, reads, writes, tok)
        return tok

    def dma(e, out, in_):
        reads, writes = regs([in_]), regs([out])
        before(e, reads, writes)
        sem = "d%d" % ndma[0]
        ndma[0] += 1
        Q[e].dma_start(ap(out), ap(in_)).then_inc(T.sem[sem], 16)
        tok = token(e, sem, 16)
        after(e, reads, writes, tok)
        return tok

    def b8(x):
        return (x[0].bitcast(dt.uint8), x[1])

    def rsend(dst, out, in_, sem):
        before("g", in_[1], [])
        nsent[0] += send(g, T, topo, core, dst, out[0], in_[0], sem)

    def arrive(sem, n, parts):
        count[sem] = n
        tok = (sem, n, {})
        last[sem] = tok
        order.append(sem)
        after("x", [], regs(parts), tok)

    def cp(o, i):
        return op("v", lambda: g.vector.tensor_copy(o[0], i[0]), [o], [i])

    def scatter(win, off, i):
        return op("v", lambda: g.vector.tensor_copy(win[0].indirect(off[0]), i[0]), [win], [i, off])

    def ts(o, i, s1, op0, s2=None, op1=None):
        if op1 is None:
            return op("v", lambda: g.vector.tensor_scalar(o[0], i[0], ap(s1), None, op0), [o], [i, s1])
        return op("v", lambda: g.vector.tensor_scalar(o[0], i[0], ap(s1), ap(s2), op0, op1), [o], [i, s1, s2])

    def tt(o, a, b, f):
        return op("v", lambda: g.vector.tensor_tensor(o[0], a[0], b[0], f), [o], [a, b])

    def scan(o, a, b, init, f0, f1):
        return op("v", lambda: g.vector.tensor_tensor_scan(o[0], a[0], b[0], ap(init), f0, f1), [o], [a, b, init])

    def total(o, i):
        return op("v", lambda: g.vector.tensor_reduce(o[0], i[0], AX.X, ALU.add), [o], [i])

    def mset(o, v):
        return op("v", lambda: g.vector.memset(o[0], v), [o], [])

    def quant(q, s, i):
        return op("v", lambda: g.vector.quantize_mx(q[0], s[0], i[0]), [q, s], [i])

    def act(o, i, f, scale=1.0, bias=None, acc=None):
        kw = {"scale": ap(scale)}
        if bias is not None:
            kw["bias"] = ap(bias)
        if acc is not None:
            kw["accum_out"] = acc[0]
        return op("s", lambda: g.scalar.activation(o[0], i[0], f, **kw), [o, acc], [i, scale, bias])

    def mm(o, w, ws, x, xs, start=True, stop=True):
        return op("t", lambda: g.tensor.matmul_mx(o[0], w[0], ws[0], x[0], xs[0], start, stop), [o], [w, ws, x, xs], adds=not start)

    def iota(o, pattern, base, step=0):
        small = {} if SCRATCH[o[1][0][0]][2] == I32 else {"allow_small_or_imprecise_dtypes": True}
        return op("g", lambda: g.iota(o[0], pattern, base, step, **small), [o], [])

    def col(k):
        return A("cols", k, k + 1)

    def bank(k, n):
        return A("psd", 512 * k, 512 * k + n)

    QC, QM1, Q4, Q4M1, B4, PG, OFF, OFF16, OFF4, OFFK, ENDK = [col(k) for k in (0, 1, 2, 6, 7, 8, 9, 10, 11, 16, 17)]

    def scan16(rowv, a=0, e=C, buf="ex16", ec="ec16"):
        scan(A(buf, a, e), rowv, A(ec, a, e), -B16, ALU.max, ALU.add)

    def list16(lst, a=0, e=C, buf="ex16"):
        ts(lst, A(buf, a + 15, e, 16), OFF16, ALU.subtract)

    def list4(lst, a, e, buf):
        ts(lst, A(buf, a + 3, e, 4), 4.0, ALU.mult, OFF4, ALU.subtract)

    def ends(a, e):
        return A("ecx", 16 * a + 15, 16 * e, 16)

    def ship(t, h):
        mine = helpers_of(T, topo, rank, t)
        if mine:
            a, e = PART[h]
            rsend(mine[VIA[h]], b8(A("rc%d" % t, a, e)), b8(A("qx%d" % t, a, e)), "hc%d_%d" % (t, h))
            rsend(mine[VIA[h]], A("rs%d" % t, a, e), A("sx%d" % t, a, e), "hs%d_%d" % (t, h))
        elif h == len(PART) - 1:
            rsend(T.cores[rank ^ STEP[t]], b8(A("lc%d" % t)), b8(A("qx%d" % t)), "ac%d" % t)
            rsend(T.cores[rank ^ STEP[t]], A("ls%d" % t), A("sx%d" % t), "ac%d" % t)

    def flags(m, a=0, e=None):
        k, j = SLOT[m]
        e = (16 * m if m else C) if e is None else e
        return A("fl", 4 * (AT[k] + a) + j, 4 * (AT[k] + e), 4)

    def pad(k):
        return 4 * (AT[k] + (16 * TILES[k][-1] if len(TILES[k]) == 4 else 0)), 4 * (AT[k] + WIDE[k])

    def scores(t, part):
        n = C if part else LOW
        for o in ([A("psa", 0, C)] + [A("psb", 0, C)] * (t > 0) if part else [bank(0, LOW), bank(1, LOW)]):
            mm(o, A("uq2"), A("us2"), A("qx%d" % t, 0, n), A("sx%d" % t, 0, n))

    def own_mask(a, e):
        tt(A("msk", a, e), A("psd" if e <= LOW else "psa", a, e), A("farq", a, e), ALU.add)

    def own_scan(a, e):
        scan(A("wsc", a, e), A("far0", a, e), A("msk", a, e), 0.0, ALU.add, ALU.min)

    dma("y", A("ut"), T.u[:])
    first = [dma(e, A("x0", 4 * a, 4 * b), T.x[:, 4 * a:4 * b]) for e, (a, b) in zip("syy", PART)]
    for tok in first:
        wait("y", tok)
    dma("y", A("vt"), T.v[:])
    dma("y", b8(A("wq")), T.wc[:])
    dma("y", A("wp"), T.ws[:])

    iota(A("pc", 0, 5), [[-1, 5]], 16, 1)
    iota(A("s32"), [[1, 64]], 0)
    iota(A("grp"), [[1, 8], [0, 16]], 1)
    iota(A("rr"), [[0, M], [1, 16]], 0)
    iota(A("jm"), [[1, C]], -H)
    mset(A("ones"), 1.0)
    op("g", lambda: g.affine_select(T.et[:], T.ones[:], [[-1, 516]], ALU.is_equal, 0.0, 3, 4), [A("et")], [A("ones")])
    mset(A("fl", *pad(0)), 0.0)
    ts(A("pc", 5, 7), A("pc", 0, 2), 15, ALU.bitwise_and)
    ts(A("pc", 7, 12), A("pc", 0, 5), 2, ALU.logical_shift_right, 3, ALU.bitwise_and)
    ts(A("pc", 12, 13), A("pc", 0, 1), 3, ALU.bitwise_and)
    ts(A("pc", 13, 14), A("pc", 0, 1), 4, ALU.logical_shift_right)
    mset(A("fl", *pad(1)), 0.0)
    ts(A("cu"), A("s32", 0, 8), 16.0, ALU.mult)
    mset(A("acc", 0, 1), 0.0)
    cp(A("cols", 0, 9), A("pc", 5, 14))
    for k in (2, 3):
        mset(A("fl", *pad(k)), 0.0)
    for k in range(NT - 1, 3, -1):
        a, e = pad(k)
        act(A("fl", a, e), A("ones", 0, e - a), ACT.Copy, scale=0.0)
    r16 = A("s32", 0, 16)
    ts(A("pat", 0, 16), r16, QC, ALU.is_equal)
    ts(A("pat", 16, 32), r16, QM1, ALU.is_equal, -2.0, ALU.mult)
    ts(A("lq"), A("s32", 0, M), 0.0, ALU.mult, QC, ALU.add)
    for k in range(8):
        ts(A("on", 512 * (k // 4) + k % 4, 512 * (k // 4 + 1), 4), A("grp"), PG, ALU.is_equal, -1.0 if k == 4 else 1.0, ALU.mult)
        if k == 3:
            tt(A("pat", 32, 48), A("pat", 0, 16), A("pat", 16, 32), ALU.add)
    act(col(12), QC, ACT.Sign)
    act(A("kp"), A("rr"), ACT.Sign)
    quant(A("uq"), A("us"), A("ut"))
    quant(A("qx0", *PART[0]), A("sx0", *PART[0]), A("x0", 2 * LOW, 4 * LOW))
    op("v", lambda: g.vector.tensor_copy(T.uq2[:, 0:128].bitcast(dt.uint32), T.uq[:, 0:128].bitcast(dt.uint32).indirect(T.cu[:, 0:8])),
       [A("uq2")], [A("uq"), A("cu")])
    op("s", lambda: g.scalar.activation(T.us2[:, 0:128], T.us[:, 0:128].indirect(T.cu[:, 0:8]), ACT.Copy), [A("us2")], [A("us"), A("cu")])
    quant(A("qx0", *PART[1]), A("sx0", *PART[1]), A("x0", 0, 2 * LOW))
    scores(0, 0)
    ts(A("farq"), A("rr"), QC, ALU.not_equal, FAR, ALU.mult)
    quant(A("qx0", LOW, C), A("sx0", LOW, C), A("x0", 4 * LOW, 4 * C))
    scores(0, 1)
    ts(A("far0"), A("rr"), 0.0, ALU.is_equal, FAR, ALU.mult)
    act(A("ec16"), ind(A("pat", 32, 48), A("lq")), ACT.Copy, scale=B16)
    act(col(13), A("pat", 47, 48), ACT.Identity, scale=B16, bias=QC)
    act(OFF16, col(12), ACT.Identity, scale=2 * B16, bias=-B16 - H)
    act(A("base", 0, M), A("jm", 0, C, 16), ACT.Identity, bias=col(13))
    c1 = LOW - 64
    own_mask(c1, LOW)
    own_mask(0, c1)
    own_scan(c1, LOW)
    for h in range(len(PART)):
        ship(0, h)

    def unpacker(b):
        quant(A("eq", 128 * b, 128 * b + 128), A("es", 128 * b, 128 * b + 128), A("et", 3 - b, 515 - b))

    spare = [[[lambda b=b: unpacker(b)] for b in range(4)]
             + [[lambda: ts(A("r4"), r16, 3, ALU.bitwise_and), lambda: ts(A("kc", 0, 4), A("s32", 0, 4), 16.0, ALU.mult, QC, ALU.add),
                 lambda: mset(A("ww", 0, 1), 0.0)],
                [lambda: ts(A("pat", 48, 64), A("r4"), Q4, ALU.is_equal), lambda: ts(A("pat", 64, 80), A("r4"), Q4M1, ALU.is_equal, -2.0, ALU.mult),
                 lambda: tt(A("ec2", 15, S, 16), A("ec2", 15, S, 16), A("kc", 0, 4), ALU.subtract)],
                [lambda: tt(A("pat", 80, 96), A("pat", 48, 64), A("pat", 64, 80), ALU.add), lambda: mset(A("se"), 0.0)]],
             [[lambda: quant(A("vq"), A("vs"), A("vt"))]]]

    for t in range(R):
        partner = T.cores[rank ^ STEP[t]]
        mine = helpers_of(T, topo, rank, t)
        theirs = helpers_of(T, topo, rank ^ STEP[t], t)
        li, ll, lc, ls = "li%d" % t, "ll%d" % t, "lc%d" % t, "ls%d" % t
        qz, sz, qf, sf = "qz%d" % t, "sz%d" % t, "qf%d" % t, "sf%d" % t
        arrive("ac%d" % t, sum(2 * len(topo.engines(k, core)) for k in ([theirs[v] for v in VIA] if theirs else [partner])), [A(lc), A(ls)])
        arrive("al%d" % t, len(topo.engines(theirs[0] if theirs else partner, core)), [A(ll, 0, M)])

        ns, nv = (NS + 1, 2 * NV) if t else (NS, NV)
        turns = list(range(NS - 1, NS - 6, -1)) + list(range(NS, ns + 1)) + list(range(NS - 6, nv, -1))
        done = [0]

        def s_first(k):
            m, o = turns[k], (k % 3) * C
            act(A("sfl", o, o + 16 * m), bank(1, 16 * m) if m <= NS else A("psb", 0, 16 * m), ACT.Sign, scale=-1.0, bias=A("wsc", 16 * m + 15, 16 * m + 16))

        def s_second(k):
            m, o = turns[k], (k % 3) * C
            act(flags(m), A("sfl", o, o + 16 * m), ACT.Relu, acc=A("acc", m, m + 1))

        def s_blocks(n):
            for k in range(done[0], done[0] + n):
                if k + 1 < len(turns):
                    s_first(k + 1)
                s_second(k)
            done[0] += n

        def v_first(m):
            ts(flags(m), A("psa" if m > NS else "psd", 0, 16 * m), A("wsc", 16 * m + 15, 16 * m + 16), ALU.is_lt)

        def v_second(m):
            if m > NS:
                e = H * (m - ns)
                scan(A("res", e - 8 * m, e), flags(m, 0, 8 * m), flags(m, 8 * m), 0.0, ALU.add, ALU.add)
            else:
                total(A("acc", m, m + 1), flags(m))

        def pack(k, start=False, stop=False):
            a, e, o = AT[k], AT[k] + WIDE[k], 0 if k else 128
            quant(A(qf, a, e), A(sf, a, e), A("fl", 4 * a, 4 * e))
            mm(A("pse", 0, e - a), A("oq", o, o + 128), A("op", o, o + 128), A(qf, a, e), A(sf, a, e), start, stop)

        s_first(0)
        s_blocks(3)
        own_scan(0, c1)
        if t == 0:
            quant(A("oq"), A("op"), A("on"))
        tt(flags(0, 0, LOW), bank(0, LOW), A("wsc", 0, LOW), ALU.is_gt)
        for m in range(nv, 0, -1):
            v_first(m)
        own_mask(LOW, C)
        scan(A("cor", 0, LOW), A("kp", 0, LOW), flags(0, 0, LOW), 0.0, ALU.mult, ALU.add)
        for m in range(1, NV + 1):
            v_second(m)
        own_scan(LOW, C)
        for m in range(NV + 1, nv + 1):
            v_second(m)
        s_blocks(len(turns) - 3)
        if t == 0:
            cp(A("ecx"), A("ec16"))
        v_first(M - 1)
        v_first(M - 2)
        tt(flags(0, LOW), A("psa", LOW, C), A("wsc", LOW, C), ALU.is_gt)
        v_first(M - 3)
        v_second(M - 1)
        v_second(M - 2)
        scan(A("cor", LOW, C), A("kp", LOW, C), flags(0, LOW), 0.0, ALU.mult, ALU.add)
        pack(0, start=True)
        v_first(M - 4)
        pack(2)
        v_first(M - 5)
        v_first(M - 6)
        pack(3)
        if ns < M - 7:
            v_first(M - 7)
        tt(A("t1", 0, M), A("base", 0, M), A("cor", 15, C, 16), ALU.add)
        pack(6)
        v_second(M - 3)
        pack(1)
        pack(4)
        for m in range(M - 4, ns + 1, -1):
            v_second(m)
        pack(5, stop=True)
        v_second(ns + 1)
        tt(ends(0, ns + 1), A("t1", 0, ns + 1), A("acc", 0, ns + 1), ALU.subtract)
        tt(ends(ns + 1, M), A("t1", ns + 1, M), A("res", H - 1, H * (M - 1 - ns), H), ALU.subtract)
        scan16(A("pse", 0, C), ec="ecx")
        list16(A(li, 0, M))
        rsend(mine[0] if mine else partner, A("rl%d" % t if mine else ll, 0, M), A(li, 0, M), ("hl%d" if mine else "al%d") % t)

        scatter(A("orow"), A(li, 0, M), A("jm"))
        if t == 0:
            iota(A("p1024"), [[int(KW), C]], 0)
            act(A("eck"), A("ec16"), ACT.Copy, scale=BIG / B16)
            act(A("ec2"), A("ec16", 0, S), ACT.Copy, scale=BIG / B16)
            act(OFF, col(12), ACT.Identity, scale=2 * BIG, bias=-BIG)
            act(OFFK, col(12), ACT.Identity, scale=2 * BIG, bias=-BIG - KW)
            act(col(14), Q4, ACT.Sign)
            act(col(15), B4, ACT.Identity, scale=-1.0, bias=-4 * (B16 + H))
            act(ENDK, A("pat", 47, 48), ACT.Identity, scale=B16, bias=OFFK)
            act(OFF4, col(14), ACT.Identity, scale=8 * B16, bias=col(15))

        tb_, kb_, bb_ = ["ta", "tb"], ["ka", "kb"], ["ba", "bb"]
        halves = [(0, MA), (MA, M)]
        act(A("tp", HA, C), ind(A("orow"), A(ll, MA, M)), ACT.Copy)
        cp(A("tp", 0, HA), ind(A("orow"), A(ll, 0, MA)))
        scan16(A("tp"))
        act(A("ba"), A("tp"), ACT.Identity, scale=KW, bias=KW * H + 2.0)
        ts(A("ka", 0, HA), A("tp", 0, HA), KW, ALU.mult, KW * H + 1.0, ALU.add)
        list16(A("lt", 0, M))
        ts(A("ka", HA, C), A("tp", HA, C), KW, ALU.mult, KW * H + 1.0, ALU.add)
        for k in range(DBL - 1):
            a, b = k % 2, (k + 1) % 2
            for c, e in halves:
                act(A(tb_[b], 16 * c, 16 * e), ind(A(tb_[a] if k else "tp"), A("lt", k * M + c, k * M + e)), ACT.Copy)
            for c, e in halves:
                tt(A(kb_[b], 16 * c, 16 * e), ind(A(bb_[a]), A("lt", k * M + c, k * M + e)), A(kb_[a], 16 * c, 16 * e), ALU.min)
            for c, e in halves:
                scan16(A(tb_[b], 16 * c, 16 * e), 16 * c, 16 * e)
            for c, e in halves:
                if c and k < len(spare[t]):
                    for f in spare[t][k]:
                        f()
                list16(A("lt", (k + 1) * M + c, (k + 1) * M + e), 16 * c, 16 * e)
            for c, e in halves:
                act(A(bb_[b], 16 * c, 16 * e), A(kb_[b], 16 * c, 16 * e), ACT.Identity, bias=float(2 ** (k + 1)))
        for b in range(4):
            mm(bank(b, C), A("eq", 128 * b, 128 * b + 128), A("es", 128 * b, 128 * b + 128), A(lc), A(ls))

        k = DBL - 1
        kn = kb_[DBL % 2]

        def leaders(a, e):
            scan(A("yy", a, e), A(kn, a, e), A("p1024", a, e), 0.0, ALU.max, ALU.max)

        def cycle_ends(a, e):
            scan(A("ww", 1 + a, 1 + e), A("yy", a, e), A("p1024", a, e), A("ww", a, a + 1), ALU.add, ALU.subtract)

        def keys(a, e):
            scan(A("exk", a, e), A(kn, a, e), A("eck", a, e), -BIG, ALU.max, ALU.add)

        def members(a, e):
            ts(A("lm", a, e), A("exk", 16 * a + 15, 16 * e, 16), OFFK, ALU.subtract, 1.0 / KW, ALU.mult)

        def leader_key(a, e):
            ts(A("t2", a, e), A("lm", a, e), KW, ALU.mult, ENDK, ALU.add)

        def steps(a, e):
            tt(ends(a, e), A("t2", a, e), A("exk", 16 * a + 15, 16 * e, 16), ALU.subtract)

        for c, e in halves:
            tt(A(kn, 16 * c, 16 * e), ind(A(bb_[k % 2]), A("lt", k * M + c, k * M + e)), A(kb_[k % 2], 16 * c, 16 * e), ALU.min)
        if t == 0:
            act(A("ec4"), ind(A("pat", 80, 96), A("lq")), ACT.Copy, scale=B16)
        leaders(0, HA)
        keys(0, HA)
        cycle_ends(0, HA)
        leaders(HA, C)
        for m in range(4):
            act(A("sj", 65 * m, 65 * m + 65), A("ww", 0, S + 1), ACT.Sign, scale=-1.0, bias=A("kc", m, m + 1), acc=A("cc", m, m + 1))
        act(A("se", 1, 2 * S + 2, 2), A("ww", 0, S + 1), ACT.Copy, scale=2.0)
        keys(HA, C)
        members(0, MA)
        cycle_ends(HA, C)
        members(MA, M)
        leader_key(0, MA)
        act(A("posr", 0, HA), ind(A("ww", 0, C + 1), A("lm", 0, MA)), ACT.Identity, bias=-float(H))
        scan(A("se", 2, 2 * S + 2, 2), A("ww", 0, S), A("ww", 1, S + 1), 0.0, ALU.min, ALU.add)
        ts(A("lcc", 0, 4), A("cc", 0, 4), float(S + 1), ALU.add)
        leader_key(MA, M)
        steps(0, MA)
        ts(A("posr", HA, C), ind(A("ww", 0, C + 1), A("lm", MA, M)), float(H), ALU.subtract)
        act(A("seg"), ind(A("se"), A("lcc", 0, 4)), ACT.Copy)
        for b in range(4):
            act(A("dp", b, 4 * C, 4), bank(b, C), ACT.Copy)
        steps(MA, M)
        scan16(A("posr", 0, HA), 0, HA, ec="ecx")
        scan16(A("posr", HA, C), HA, C, ec="ecx")
        scan(A("ex2"), A("seg"), A("ec2"), -BIG, ALU.max, ALU.add)
        list16(A("lp", 0, MA), 0, HA)
        list16(A("lp", MA, M), HA, C)
        ts(A("lk", 0, 4), A("ex2", 15, S, 16), OFF, ALU.subtract)
        scatter(A("erow"), A("lp"), A("jm"))

        banks = [[bank(b, PART[h][1] - PART[h][0]) for b in range(4)] for h in (0, 1)]
        banks.append([A(n, 0, C - LOW) for n in ("psa", "psb", "pse", "psf")])
        xo, xn, nx, ns_ = "x%d" % t, "x%d" % (t + 1), "qx%d" % (t + 1), "sx%d" % (t + 1)
        outs = [None, (0, LOW), (LOW, C)]

        def run(name, h):
            return A(name, 4 * PART[h][0], 4 * PART[h][1])

        def tile(name, h, b):
            return A(name, 4 * PART[h][0] + b, 4 * PART[h][1], 4)

        def words(a, e):
            scan16(A("erow", a, e), a, e, "ex4", "ec4")

        def offsets(a, e):
            list4(A("le", a // 4, e // 4), a, e, "ex4")

        def own_v(a, e):
            cp(A("z", 4 * a, 4 * e), ind(A(xo), A("le", a // 4, e // 4)))

        def own_s(a, e):
            act(A("z", 4 * a, 4 * e), ind(A(xo), A("le", a // 4, e // 4)), ACT.Copy)

        def products(h, bs):
            a, e = PART[h]
            for b in bs:
                mm(banks[h][b], A("wq", 128 * b, 128 * b + 128), A("wp", 128 * b, 128 * b + 128), A(qz, a, e), A(sz, a, e))

        def layer(h, bs=range(4)):
            a, e = PART[h]
            quant(A(qz, a, e), A(sz, a, e), run("z", h))
            products(h, bs)

        def finish(h):
            a, e = PART[h]
            quant(A(nx, a, e), A(ns_, a, e), run(xn, h))
            if t < R - 1:
                if h:
                    scores(t + 1, h - 1)
                ship(t + 1, h)
            elif h:
                a, e = outs[h]
                mm(bank(h, e - a), A("vq"), A("vs"), A(nx, a, e), A(ns_, a, e))
                dma("y", T.oc[:, 4 * a:4 * e], b8(A(nx, a, e)))

        def store(h):
            a, e = outs[h]
            act(A("ybuf", a, e), bank(h, e - a), ACT.Copy)
            dma("s", T.y[:, a:e], A("ybuf", a, e))

        def scales(e, ks):
            for k in ks:
                dma(e, T.osc[4 * k:4 * k + 4, :], (T[ns_][32 * k:32 * k + 4, :], A(ns_)[1]))

        def up_v(h, bs=None):
            for o, i in ([(run("z64", h), run("z", h))] if bs is None else [(tile("z64", h, b), tile("z", h, b)) for b in bs]):
                ts(o, i, 64.0, ALU.mult)

        def up_s(h, bs):
            for b in bs:
                act(tile("z64", h, b), tile("z", h, b), ACT.Copy, scale=64.0)

        def down_v(h, bs):
            for b in bs:
                ts(tile(xn, h, b), tile("xs", h, b), 1.0 / 64.0, ALU.mult)

        def down_s(h, bs):
            for b in bs:
                act(tile(xn, h, b), tile("xs", h, b), ACT.Copy, scale=1.0 / 64.0)

        def add(h, bs=range(4)):
            for b in bs:
                tt(tile("xs", h, b), banks[h][b], tile("z64", h, b), ALU.add)

        a0, mid = PART[0][0], (PART[0][0] + LOW) // 2
        words(a0, LOW)
        act(A("e3r"), ind(A("erow"), A("lk", 0, 4)), ACT.Copy)
        words(S, a0)
        offsets(a0, LOW)
        offsets(S, a0)
        scan16(A("e3r"), 0, S, "ex17", "ec4")
        own_s(mid, LOW)
        own_v(a0, mid)
        words(LOW, C)
        list4(A("le3"), 0, S, "ex17")
        own_s(S, a0)
        act(A("z", 0, 4 * S), ind(A("dp"), A("le3")), ACT.Copy)
        layer(0)
        offsets(LOW, C)
        up_v(0)
        own_s(LOW, LOW + 64)
        add(0, (0, 1))
        layer(1, (0, 1))
        up_s(1, (2, 3))
        own_s(LOW + 64, C)
        add(0, (2,))
        products(1, (2,))
        up_v(1, (0, 1))
        add(0, (3,))
        products(1, (3,))
        down_v(0, (0, 1))
        down_s(0, (2, 3))
        add(1)
        layer(2)
        down_s(1, (0, 2))
        down_v(1, (1, 3))
        up_s(2, range(4))
        finish(0)
        finish(1)
        add(2)
        if t == R - 1:
            act(A("elf"), A("erow"), ACT.Identity, bias=float(H))
            dma("y", T.el[:], (T.elf[0:128:16, :], A("elf")[1]))
            down_s(2, (2,))
            store(1)
            down_v(2, (0, 1, 3))
            finish(2)
            scales("s", (0, 1))
            scales("y", (2, 3))
            store(2)
        else:
            down_v(2, (0, 1))
            down_s(2, (2, 3))
            own_mask(c1, LOW)
            own_mask(0, c1)
            own_scan(c1, LOW)
            finish(2)

    g.wait_ge(T.sem["sent"], nsent[0])
    seen = set()
    final = []
    for sem in reversed(order):
        if sem not in seen:
            seen.add(sem)
            final.append(sem)
    for sem in reversed(final):
        if waited.get(sem, 0) < count[sem]:
            g.wait_ge(T.sem[sem], count[sem])
